import numpy as np, ml_dtypes
CORES = [3,7,11,15,131,135,139,143]
N = 8
import mx_ref
BF = ml_dtypes.bfloat16
def gentries(a):
    return np.ascontiguousarray(a.reshape(8, 16, -1).transpose(0, 2, 1)).reshape(8, -1)
def gtable(e):
    e = np.asarray(e); return np.ascontiguousarray(e.reshape(8, -1, 16).transpose(0, 2, 1)).reshape(128, -1).astype(np.int32)
def gcols(t, e):
    v = np.concatenate([t.reshape(8, 16, -1, 4), np.zeros((8, 16, 1, 4), BF)], axis=2)
    return np.ascontiguousarray(np.stack([v[g][:, e[g]] for g in range(8)])).reshape(128, -1)
def tile(rs):
    return np.stack(rs, axis=2).reshape(128, -1).astype(BF)
def pick(q, e):
    c = np.concatenate([q[0].reshape(128, -1, 4), np.zeros((128, 1, 4), np.uint8)], axis=1); s = np.concatenate([q[1], np.ones((16, 1), np.uint8)], axis=1)
    return (np.ascontiguousarray(c[:, e].reshape(128, -1)), np.ascontiguousarray(s[:, e]))
def join(*qs):
    return (np.concatenate([q[0] for q in qs], axis=1), np.concatenate([q[1] for q in qs], axis=1))
def put(q, e, v):
    c, s = q[0].reshape(128, -1, 4).copy(), q[1].copy(); c[:, e] = v[0].reshape(128, -1, 4); s[:, e] = v[1]
    return (c.reshape(128, -1), s)
def pk(c, s):
    return (np.ascontiguousarray(c), mx_ref.live(s))
def emit(q):
    return q[0], q[1]
def packed(v, rng):
    q = [mx_ref.quantize(np.ascontiguousarray(v[r])) for r in range(N)]
    return np.stack([a for a, b in q]), np.stack([mx_ref.plane(b, rng) for a, b in q])
def values_of_codes():
    e, c = np.zeros((128, 128, 4), np.float32), np.zeros((128, 2, 4), np.uint8)
    e[np.arange(128), np.arange(128), 0] = 1
    c[:127, :, 0] = np.arange(256).reshape(2, 128).T[:127]
    return mx_ref.matmul(mx_ref.quantize(e.reshape(128, 512).astype(BF)), (c.reshape(128, 8), np.full((16, 2), 127, np.uint8))).T.reshape(-1).astype(np.float64)
CODE_VALUE, SCALE_VALUE = values_of_codes(), 2.0 ** (np.arange(256) - 127.0)
def decode(q):
    return (CODE_VALUE[q[0]].reshape(16, 8, -1, 4) * SCALE_VALUE[q[1]][:, None, :, None] + 0.0).reshape(128, -1).astype(np.float32)
def f(rng, *shape):
    return mx_ref.flush((rng.standard_normal(shape, dtype=np.float32) * np.exp2(rng.integers(-2, 3, shape[:-1] + (1,)))).astype(BF))
def wide(rng, *shape, cols=0):
    v = rng.standard_normal(shape, dtype=np.float32) * np.exp2(rng.integers(-12, 13, shape)).astype(np.float32)
    if cols: v *= np.repeat(np.exp2(rng.integers(-cols, cols + 1, shape[:-2] + (1, shape[-1] // 4))) * (rng.random(shape[:-2] + (1, shape[-1] // 4)) > 0.0625), 4, axis=-1).astype(np.float32)
    return mx_ref.flush(v.astype(BF))
C, HALF, E = 288, 144, 224
MASK = [4, 1, 2]
TIMES = 9
def register(b):
    a = 2 * np.arange(HALF)
    return np.concatenate([a + b, a + 1 - b], axis=-1)
def lowest(s):
    low, to = np.broadcast_to(np.arange(C), s.shape), s
    for i in range(TIMES):
        low = np.minimum(low, np.take_along_axis(low, to, axis=-1))
        to = np.take_along_axis(to, to, axis=-1)
    return low
def joined(s):
    low, c = lowest(s), np.arange(HALF)
    a, b = low[..., :HALF], low[..., HALF:]
    swap = (a != b) & ((a == c) & (c > 0) | (b == c + HALF))
    return np.concatenate([np.where(swap, s[..., HALF:], s[..., :HALF]), np.where(swap, s[..., :HALF], s[..., HALF:])], axis=-1)
def numbers_of(rng):
    return {"x": np.array(f(rng, N, 128, 4 * C)), "u": np.array(f(rng, N, 128, 512)), "v": np.array(f(rng, N, 128, 512))}
def orders(rng):
    return rng.permuted(np.tile(np.arange(C), (N, 8, 1)), axis=2)
def stored(k):
    return {"kl": np.stack([gtable(k[r]) for r in range(N)])}
def layers(rng):
    return np.array(f(rng, N, 128, 2048)).reshape(N, 8, 16, 4, 8, 16, 4)
def weights(rng, w):
    c, p = packed(np.ascontiguousarray(w).reshape(N, 128, 2048), rng)
    return {"wc": c, "ws": p}
def setup_inputs(rng):
    return {**numbers_of(rng), **stored(orders(rng)), **weights(rng, layers(rng))}
def setup_inputs_ties(rng):
    d = numbers_of(rng)
    o = rng.permutation(N)
    k = rng.integers(-1, 2, (N, 8, C)).astype(np.float32)
    k[o[1]] = 1
    x = d["x"].reshape(N, 8, 16, C, 4)
    x[:, :, 0] = 0
    x[:, :, 0, :, 0] = k.astype(BF)
    a = np.exp2(rng.integers(-3, 4, (8, 1)).astype(np.float64))
    j = rng.integers(3, 7, (8, 4, 6))
    j[:, :, 0] = 6
    q = (9 + 2 * rng.integers(0, 4, (8, 4, 6))) * 0.125 * np.exp2(-j.astype(np.float64))
    x[:, :, 8:] = 0
    x[:, :, 8, :, 0] = (-3.0 * a).astype(np.float32).astype(BF)
    x[:, :, 10, :, 0] = (-0.140625 * a).astype(np.float32).astype(BF)
    x[:, :, 10, :, 1] = (-0.125 * a).astype(np.float32).astype(BF)
    c = np.ones(N, np.float32)
    c[o[0]] = 0
    c[o[2]] = -1
    u = d["u"].reshape(N, 128, 128, 4)
    u[:, :, ::16] = 0
    for h in range(0, 128, 16): u[:, h, h, 0] = c.astype(BF)
    w = layers(rng)
    w[:, :, 0] = 0
    w[:, :, :, :, :, 0] = 0
    w[:, :, :, :, :, 8:] = 0
    for g in range(8): w[:, g, 10, 0, g, 8, 0] = -224.0
    for n, i in enumerate((9, 11, 12, 13, 14, 15)):
        x[:, :, i] = (q[:, :, n] * a * -0.0078125)[:, None].astype(np.float32).astype(BF)
        for g in range(8): w[:, g, 10, :, g, i, 1] = (-q[g, :, n]).astype(np.float32).astype(BF)
    return {"x": x.reshape(N, 128, 4 * C), "u": u.reshape(N, 128, 512), "v": d["v"], **stored(orders(rng)), **weights(rng, w)}
def setup_inputs_near(rng):
    d = numbers_of(rng)
    o = rng.permutation(N) % 4
    k = np.where((o == 1) | (o == 2), 1.0, 2.0 ** -30).astype(np.float32)
    x = d["x"].astype(np.float32).reshape(N, 8, 16, C, 4)
    x[:, :, :8] = 0
    s = rng.integers(-1, 2, (N, 8, C)) * k[:, None, None]
    s[o == 3] = 0
    x[:, :, 0, :, 0] = 1.125 * s
    x[:, :, 1, :, 0] = -1.25 * s
    x[:, :, 7, :, 0] = 2.0 ** -30
    w = layers(rng)
    w[:, :, :8] = 0
    w[:, :, :, :, :, :8] = 0
    for r in range(N):
        if o[r] == 3:
            x[r, :, 4, :, 0] = rng.choice([-1.0, 1.0], (8, C)) * 2.0 ** -30
            for g in range(8):
                w[r, g, 4, 0, g, 0, 0] = 1.125 * 2.0 ** -8
                w[r, g, 4, 0, g, 1, 0] = -1.25 * 2.0 ** -8
                w[r, g, 7, 0, g, 6, 0] = 2.0 ** 5
        at = [0, C - 1, int(rng.integers(C)), int(rng.integers(C))]
        for g, j in zip(rng.permutation(8)[:4], at): x[r, g, 0, j, 0] = 2.0 ** 30 * rng.choice([-1.0, 1.0])
    u = d["u"].reshape(N, 128, 128, 4)
    u[:, :, ::16] = 0
    for h in range(0, 128, 16):
        u[:, h, h, 0] = (1.125 * k).astype(np.float32).astype(BF)
        u[:, h + 1, h, 0] = k.astype(BF)
    return {"x": x.reshape(N, 128, 4 * C).astype(BF), "u": u.reshape(N, 128, 512), "v": d["v"], **stored(orders(rng)), **weights(rng, w)}
def setup_inputs_long(rng):
    d = numbers_of(rng)
    k = orders(rng)
    b = rng.integers(0, 2, (N, 8, HALF))
    for c in rng.permutation(HALF):
        low = lowest(register(b))
        b[..., c] ^= (low[..., c] != low[..., c + HALF]).astype(np.int64)
    last = HALF - 1 - (HALF - 1) // 2
    way = [last >> i for i in range(last.bit_length() - 1, -1, -1)]
    for r in range(N):
        t = rng.permutation(8)
        for g in t[2:4]: b[r, g, rng.integers(1, HALF)] ^= 1
        b[r, t[4], 0] ^= 1
        for g in t[5:]: b[r, g] = rng.integers(0, 2, HALF)
        for g in t[5:7]:
            b[r, g, HALF - 1] = 0
            for i, j in zip(way, way[1:]): b[r, g, HALF - 1 - i] = j & 1
            b[r, g, HALF - 1 - last] = 1 - (HALF - 1) % 2
    s = np.zeros((N, 8, C))
    np.put_along_axis(s, k, np.concatenate([b, rng.integers(0, 2, (N, 8, HALF))], axis=2) * 2.0 - 1.0, axis=2)
    x = d["x"].reshape(N, 8, 16, C, 4)
    x[:, :, 0] = 0
    x[:, :, 0, :, 0] = (s * np.exp2(rng.integers(-3, 4, (N, 8, C)).astype(np.float64))).astype(np.float32).astype(BF)
    u = d["u"].reshape(N, 128, 128, 4)
    u[:, :, ::16] = 0
    for h in range(0, 128, 16): u[:, h, h, 0] = 1
    w = layers(rng)
    w[:, :, :, :, :, 0] = (w[:, :, :, :, :, 0].astype(np.float32) * 4).astype(BF)
    return {"x": x.reshape(N, 128, 4 * C), "u": u.reshape(N, 128, 512), "v": d["v"], **stored(k), **weights(rng, w)}
def setup_inputs_ends(rng):
    d = numbers_of(rng)
    o, e = rng.permutation(N) % 4, rng.permutation(N) % 4
    k = orders(rng)
    x = np.zeros((N, 8, 16, C, 4))
    u = d["u"].astype(np.float32).reshape(N, 128, 128, 4)
    v = np.zeros((N, 128, 512))
    w = np.zeros((N, 128, 4, 128, 4), np.float32)
    i = np.arange(128)[np.arange(128) % 16 < 15]
    j = np.arange(14, 128, 16)
    up, down = np.arange(C), np.arange(C)[::-1]
    for r in range(N):
        if e[r] == 0: k[r] = up
        if e[r] == 1: k[r] = down
        if e[r] == 2: k[r] = np.where(rng.permutation(8)[:, None] < 4, up, down)
        h = rng.permutation(8)
        c = np.where(h < 2, 0.0, h % 2 * 2.0 - 1.0)[None, :, None]
        much = (0.9 + 0.1 * rng.random((8, 16, C, 4))) * 2.0 ** 29
        if o[r] == 0: x[r] = -much
        if o[r] == 1: x[r] = much * rng.choice([-1.0, 1.0], (1, 1, C, 1))
        if o[r] == 2: x[r] = -(1.0 + 0.125 * rng.integers(0, 8, (8, 16, C, 4))) * 2.0 ** -30
        if o[r] == 3: x[r] = d["x"][r].astype(np.float32).reshape(8, 16, C, 4)[:, :, :1]
        x[r, :, 15] = 2.0 ** -30
        if o[r] < 2:
            u[r, :, ::16] = c * (0.9 + 0.1 * rng.random((128, 8, 4))) * 2.0 ** 30
            v[r] = (0.9 + 0.1 * rng.random((128, 512))) * 2.0 ** 30
        else:
            v[r] = (1.0 + 0.125 * rng.integers(0, 8, (128, 512))) * 2.0 ** -30
        if o[r] == 2: u[r, :, ::16] = c * (1.0 + 0.125 * rng.integers(0, 8, (128, 8, 4))) * 2.0 ** -30
        if o[r] == 3: u[r, :, ::16] *= np.abs(c).astype(np.float32)
        n = np.array([1.0, 2.0, 4.0])[rng.permutation(8) % 3]
        for b in range(4):
            if o[r] != 2: w[r, i, b, i, b] = -n[i // 16]
            else:
                w[r, i, b, i, b] = -2.0 ** -8
                w[r, j, b, j, b] = 0.0
                w[r, j + 1, b, j, b] = 2.0 ** 8
                w[r, j - 8, b, j - 8, b] = 0.0
                w[r, j + 1, b, j - 8, b] = 2.0 ** 5
    v = v * rng.choice([-1.0, 1.0], (N, 128, 512))
    return {"x": x.astype(np.float32).reshape(N, 128, 4 * C).astype(BF), "u": u.reshape(N, 128, 512).astype(BF), "v": v.astype(np.float32).astype(BF), **stored(k), **weights(rng, w.astype(BF))}
def setup_inputs_spread(rng):
    d = setup_inputs(rng)
    d["x"] = wide(rng, N, 128, 4 * C, cols=6)
    return d
def check_inputs(d):
    b = []
    for k in ("x", "u", "v"):
        a = np.abs(d[k].astype(np.float32))
        if not (np.isfinite(a).all() and ((a == 0) | (a >= 2.0 ** -30) & (a <= 2.0 ** 30)).all()): b.append("a value of " + k)
    none, least, most = [emit(mx_ref.quantize(np.full((128, 16), k, np.float32).astype(BF)))[1][0, 0] for k in (0.0, 2.0 ** -8, 2.0 ** 8)]
    for r in range(N):
        if not (np.sort(gentries(d["kl"][r]), axis=1) == np.arange(C)).all(): b.append("kl: not a permutation")
        if ((d["wc"][r] == 0x7F) | (d["wc"][r] == 0xFF)).any(): b.append("wc: a code that is no number")
        s = mx_ref.live(d["ws"][r])
        if ((s != none) & ((s < least) | (s > most))).any(): b.append("ws: a scale out of range")
    return b
def reference(x, u, v, kl, wc, ws):
    qu = [mx_ref.quantize(u[r]) for r in range(N)]
    lay = [pk(wc[r], ws[r]) for r in range(N)]
    now = [x[r] for r in range(N)]
    k = [gentries(kl[r]).astype(np.int64) for r in range(N)]
    for m in MASK:
        e, made = [], []
        for r in range(N):
            s = mx_ref.matmul(qu[r], mx_ref.quantize(now[r]))[::16]
            bits = (np.take_along_axis(s, k[r][:, :HALF], axis=1) > 0).astype(np.int64)
            e.append(np.take_along_axis(k[r], joined(register(bits)), axis=1))
            z = (gcols(now[r], k[r]).astype(np.float32) + gcols(now[r], e[r]).astype(np.float32)) * np.float32(0.5)
            q = mx_ref.quantize(z.astype(BF))
            made.append(tile([mx_ref.matmul(pick(lay[r], np.arange(128 * b, 128 * b + 128)), q) * np.float32(0.03125) for b in range(4)]))
        k = [np.take_along_axis(k[r ^ m], e[r], axis=1) for r in range(N)]
        for r in range(N):
            far = decode(mx_ref.quantize(np.ascontiguousarray(made[r ^ m][:, :4 * E]))).astype(BF)
            both = np.concatenate([far, made[r][:, 4 * E:]], axis=1)
            now[r] = (now[r].astype(np.float32) + gcols(both, k[r]).astype(np.float32)).astype(BF)
    y, kp = np.zeros((N, 128, C), np.float32), np.zeros((N, 8, C), np.float32)
    oc, osc = np.zeros((N, 128, 4 * C), np.uint8), np.zeros((N, 16, C), np.uint8)
    for r in range(N):
        q = mx_ref.quantize(now[r])
        y[r] = mx_ref.matmul(mx_ref.quantize(v[r]), q)
        kp[r] = k[r]
        oc[r], osc[r] = emit(q)
    return {"y": y, "kp": kp, "oc": oc, "osc": osc}

@@ -1,0 +1,530 @@
+from concourse.bass import DstId, RemoteDMATransfer
+from concourse.mybir import dt, AluOpType, AxisListType, ActivationFunctionType
+
+C, HALF, E = 288, 144, 224
+MASKS = [4, 1, 2]
+C1 = 144
+C2 = E - C1
+F4 = "float8_e4m3fn_x4"
+
+SCRATCH = {
+    "ub": ("sbuf", [128, 512], "bfloat16"), "vb": ("sbuf", [128, 512], "bfloat16"), "et": ("sbuf", [128, 2048], "bfloat16"),
+    "one": ("sbuf", [128, 512], "bfloat16"),
+    "uq": ("sbuf", [128, 128], F4), "us": ("sbuf", [128, 128], "uint8"),
+    "ur": ("sbuf", [128, 128], F4), "urs": ("sbuf", [128, 128], "uint8"),
+    "vq": ("sbuf", [128, 128], F4), "vs": ("sbuf", [128, 128], "uint8"),
+    "eq": ("sbuf", [128, 512], F4), "es": ("sbuf", [128, 512], "uint8"),
+    "wq": ("sbuf", [128, 512], F4), "wp": ("sbuf", [128, 512], "uint8"),
+    "kli": ("sbuf", [128, 18], "int32"), "ki": ("sbuf", [128, 54], "int32"),
+    "kld": ("dram", [128, 18], "int32"), "lk0": ("dram", [128, 18], "int32"),
+    "nd1": ("dram", [128, 18], "float32"), "nd2": ("dram", [128, 18], "float32"),
+    "lk1": ("dram", [128, 18], "float32"), "lk2": ("dram", [128, 18], "float32"),
+    "kf0": ("sbuf", [128, C], "int32"), "kf1": ("sbuf", [128, C], "float32"), "kf2": ("sbuf", [128, C], "float32"),
+    "pI": ("sbuf", [128, 8], "int32"), "uI": ("sbuf", [128, 8], "int32"), "pF": ("sbuf", [128, 24], "float32"),
+    "uo": ("sbuf", [128, 8], "uint16"),
+    "ks": ("sbuf", [128, 18], "uint16"), "k4t": ("sbuf", [128, 80], "uint16"),
+    "oAD": ("sbuf", [128, 10], "uint16"), "oBC": ("sbuf", [128, 10], "uint16"), "oRi": ("sbuf", [128, 6], "uint16"),
+    "o4": ("sbuf", [128, 4], "uint16"), "oVC": ("sbuf", [128, 6], "uint16"), "oR": ("sbuf", [128, 6], "uint16"),
+    "tt4": ("sbuf", [128, 72], "uint16"), "tt18": ("sbuf", [128, 18], "uint16"),
+    "ps": ("psum", [128, 4096], "float32"),
+    "ysb": ("sbuf", [128, C], "float32"),
+}
+for _i in range(4):
+    SCRATCH["X%d" % _i] = ("sbuf", [128, 4 * C], "bfloat16")
+    SCRATCH["xq%d" % _i] = ("sbuf", [128, C], F4)
+    SCRATCH["xs%d" % _i] = ("sbuf", [128, C], "uint8")
+    SCRATCH["oP%d" % _i] = ("sbuf", [128, 6], "uint16")
+    SCRATCH["kt%d" % _i] = ("sbuf", [128, 18], "uint16")
+for _i in range(3):
+    SCRATCH["XK%d" % _i] = ("sbuf", [128, 4 * C], "bfloat16")
+    SCRATCH["XC%d" % _i] = ("sbuf", [128, 4 * C], "bfloat16")
+    SCRATCH["Z%d" % _i] = ("sbuf", [128, 4 * C], "bfloat16")
+    SCRATCH["H%d" % _i] = ("sbuf", [128, 4 * E], "bfloat16")
+    SCRATCH["B%d" % _i] = ("sbuf", [128, 4 * C], "bfloat16")
+    SCRATCH["zq%d" % _i] = ("sbuf", [128, C], F4)
+    SCRATCH["zs%d" % _i] = ("sbuf", [128, C], "uint8")
+    SCRATCH["hq%d" % _i] = ("sbuf", [128, C1 + 128], F4)
+    SCRATCH["hs%d" % _i] = ("sbuf", [128, C1 + 128], "uint8")
+    SCRATCH["lq%d" % _i] = ("sbuf", [128, E], F4)
+    SCRATCH["ls%d" % _i] = ("sbuf", [128, E], "uint8")
+    SCRATCH["nt%d" % _i] = ("sbuf", [128, 72], "uint16")
+    SCRATCH["nf%d" % _i] = ("sbuf", [128, C], "float32")
+    SCRATCH["kk%d" % _i] = ("sbuf", [128, C], "float32")
+_ROWS = {
+    "t16": 288, "t4": 288, "t8": 80, "t2": 80, "J": 80, "q16": 16, "q32": 40,
+    "W1": 288, "W2": 288, "W3": 288, "W4": 288, "cAD": 144, "sgM": 144, "M16n": 288, "M4n": 288, "M2": 80, "M8": 80,
+    "m16z": 288, "m8z": 80, "m4z": 288, "d16": 288, "d4": 288, "JM2": 80, "JM8": 80,
+    "cT": 16, "tA": 16, "tB": 16, "tC": 16, "tD": 16, "tcAD": 16, "tcBC": 16, "sgT": 16, "tb": 24, "b1": 40, "b2": 40,
+    "bits": 288, "fl": 144, "w": 144, "sc": 144, "AD": 16, "BC": 16, "tw": 32, "ts": 32, "tm": 32,
+    "Vw": 80, "Vs": 80, "Vb": 80, "Pw": 80, "Ps": 80, "F0": 80, "F1": 80, "F2": 80, "G0": 80, "G1": 80, "G2": 80,
+    "Gw": 80, "Gs": 80, "l0": 80, "l1": 80, "l2": 80, "l3": 80, "l4": 80, "l5": 80, "l6": 80, "l7": 80, "lc": 80,
+    "Rw": 80, "Rs": 80, "fM4": 144, "fS4": 144, "fM2": 80, "dn": 40, "dj": 40, "s1": 40, "fs": 40, "dh": 40, "c1": 40, "c2": 40,
+    "a": 80, "b": 80, "cd": 80, "dc": 40, "dy": 40, "tab": 72,
+    "fM8": 80, "fS8": 80, "a8": 80, "c8": 80, "cS8": 80, "f18": 16, "s18": 16, "fs18": 16, "h18": 16, "dy18": 16, "tab18": 24,
+    "n4w": 288, "n4s": 288, "n16w": 288, "n16s": 288,
+}
+OFF = {}
+_n = 0
+for _k, _v in _ROWS.items():
+    OFF[_k] = _n
+    _n += (_v + 7) // 8 * 8
+SCRATCH["F"] = ("sbuf", [128, _n], "float32")
+
+SEMAPHORES = ["v", "s", "p", "q", "sent", "dx0", "dx1", "dk", "du", "dw", "dv", "dkl", "dn1", "dn2", "df0", "df1", "df2", "dout",
+              "lr0", "lr1", "lr2", "ha0", "ha1", "ha2", "hb0", "hb1", "hb2"]
+
+
+def rank_program(g, core, T, topo):
+    rank = T.rank_of(core)
+    if rank is None:
+        return
+    A = AluOpType
+    COPY = ActivationFunctionType.Copy
+    queue = {"v": g.vector, "s": g.scalar, "p": g.tensor, "q": g, "y": g.sync}
+    total, known, log = {}, {}, {}
+
+    def f(name, a=0, b=None, step=1):
+        o = OFF[name]
+        return ("F", o + a, o + (_ROWS[name] if b is None else b), step)
+
+    def t(name, a=0, b=None, step=1):
+        return (name, a, SCRATCH[name][1][1] if b is None else b, step)
+
+    def ap(x):
+        return T[x[0]][:, x[1]:x[2]:x[3]] if x[3] != 1 else T[x[0]][:, x[1]:x[2]]
+
+    def ind(win, off):
+        return ap(win).indirect(ap(off))
+
+    def clash(x, y):
+        if x[0] != y[0] or x[1] >= y[2] or y[1] >= x[2]:
+            return False
+        if x[3] == y[3] and x[3] > 1 and (x[1] - y[1]) % x[3]:
+            return False
+        return True
+
+    def need(q, sem, val):
+        if known.get((q, sem), 0) < val:
+            queue[q].wait_ge(T.sem[sem], val)
+            known[(q, sem)] = val
+
+    def order(q, reads, writes):
+        want = {}
+        for rw, views in ((0, reads), (1, writes)):
+            for x in views:
+                for y, w, sem, val in log.get(x[0], ()):
+                    if (rw or w) and clash(x, y):
+                        want[sem] = max(want.get(sem, 0), val if val else total[sem])
+        for sem in want:
+            need(q, sem, want[sem])
+
+    def note(sem, val, reads, writes):
+        for x in writes:
+            log[x[0]] = [e for e in log.get(x[0], []) if not (e[0][1] >= x[1] and e[0][2] <= x[2] and (x[3] == 1 or x == e[0]))]
+            log[x[0]].append((x, 1, sem, val))
+        for x in reads:
+            log.setdefault(x[0], []).append((x, 0, sem, val))
+
+    def run(q, call, reads, writes):
+        psum = [("ps", x[1] // 512 * 512, x[1] // 512 * 512 + 512, 1) for x in reads + writes if x[0] == "ps"]
+        reads, writes = [x for x in reads if x[0] != "ps"], [x for x in writes if x[0] != "ps"] + psum
+        order(q, reads, writes)
+        total[q] = total.get(q, 0) + 1
+        call().then_inc(T.sem[q], 1)
+        note(q, total[q], reads, writes)
+
+    def dma(q, sem, out, in_, reads, writes):
+        order(q, reads, writes)
+        total[sem] = total.get(sem, 0) + 16
+        queue[q].dma_start(out, in_).then_inc(T.sem[sem], 16)
+        note(sem, 0, reads, writes)
+
+    def tt(out, a, b, op):
+        run("v", lambda: g.vector.tensor_tensor(ap(out), ap(a), ap(b), op), [a, b], [out])
+
+    def ts(out, a, s1, op0, s2=None, op1=None):
+        sc = [x for x in (s1, s2) if isinstance(x, tuple)]
+        u1 = ap(s1) if isinstance(s1, tuple) else s1
+        u2 = ap(s2) if isinstance(s2, tuple) else s2
+        if op1 is None:
+            run("v", lambda: g.vector.tensor_scalar(ap(out), ap(a), u1, None, op0), [a] + sc, [out])
+        else:
+            run("v", lambda: g.vector.tensor_scalar(ap(out), ap(a), u1, u2, op0, op1), [a] + sc, [out])
+
+    def cp(out, a):
+        run("v", lambda: g.vector.tensor_copy(ap(out), ap(a)), [a], [out])
+
+    def gat(out, win, off):
+        run("v", lambda: g.vector.tensor_copy(ap(out), ind(win, off)), [win, off], [out])
+
+    def gop(out, win, off, b, op):
+        run("v", lambda: g.vector.tensor_tensor(ap(out), ind(win, off), ap(b), op), [win, off, b], [out])
+
+    def scan(out, d0, d1, op0, op1):
+        run("v", lambda: g.vector.tensor_tensor_scan(ap(out), ap(d0), ap(d1), 0.0, op0, op1), [d0, d1], [out])
+
+    def act(out, a, scale=1.0):
+        run("s", lambda: g.scalar.activation(ap(out), ap(a), COPY, scale=scale), [a], [out])
+
+    def acts(out, a, col):
+        run("s", lambda: g.scalar.activation(ap(out), ap(a), COPY, scale=ap(col)), [a, col], [out])
+
+    def actf(out, a, func, scale, bias):
+        if isinstance(bias, tuple):
+            run("s", lambda: g.scalar.activation(ap(out), ap(a), func, bias=ap(bias), scale=scale), [a, bias], [out])
+        else:
+            run("s", lambda: g.scalar.activation(ap(out), ap(a), func, bias=bias, scale=scale), [a], [out])
+
+    def equal(out, a, col, tmp):
+        actf(tmp, a, ActivationFunctionType.Abs, -1.0, col)
+        actf(out, tmp, ActivationFunctionType.Relu, -1.0, 1.0)
+
+    def actg(out, win, off, scale=1.0):
+        run("s", lambda: g.scalar.activation(ap(out), ind(win, off), COPY, scale=scale), [win, off], [out])
+
+    def quant(q, s, a):
+        run("v", lambda: g.vector.quantize_mx(ap(q), ap(s), ap(a)), [a], [q, s])
+
+    def mm(out, l, ls, r, rs):
+        run("p", lambda: g.tensor.matmul_mx(ap(out), ap(l), ap(ls), ap(r), ap(rs), True, True), [l, ls, r, rs], [out])
+
+    def iota(out, pattern, base=0, cm=0):
+        if out[0] == "F":
+            run("q", lambda: g.iota(ap(out), pattern, base, cm, allow_small_or_imprecise_dtypes=True), [], [out])
+        else:
+            run("q", lambda: g.iota(ap(out), pattern, base, cm), [], [out])
+
+    def bank(i, n):
+        i %= 8
+        return ("ps", 512 * i, 512 * i + n, 1)
+
+    def send(dst, sem, out, in_, reads, bits=False):
+        order("q", reads, [])
+        rid, pid = topo.addr(dst, core)
+        n = len(topo.engines(core, dst))
+        o, i = (ap(out).bitcast(dt.uint8), ap(in_).bitcast(dt.uint8)) if bits else (ap(out), ap(in_))
+        if SCRATCH[out[0]][0] == "dram":
+            o, i = T[out[0]][:, :], T[in_[0]][:, :]
+        total["sent"] = total.get("sent", 0) + n
+        g.remote_dma(o, i, T.sem[sem], T.sem.sent, pid, rid, topo.mask(core, dst))
+        return n
+
+    def arrives(sem, n, writes):
+        total[sem] = total.get(sem, 0) + n
+        note(sem, 0, [], writes)
+
+    dma("y", "dx0", T.X0[:, 0:576], T.x[:, 0:576], [], [t("X0", 0, 576)])
+    dma("s", "dk", T.kli[:, :], T.kl[:, :], [], [t("kli")])
+    dma("s", "du", T.ub[:, :], T.u[:, :], [], [t("ub")])
+    dma("y", "dx1", T.X0[:, 576:1152], T.x[:, 576:1152], [], [t("X0", 576, 1152)])
+    dma("y", "dkl", T.kld[:, :], T.kl[:, :], [], [t("kld")])
+    dma("y", "dw", T.wq[:, 0:512].bitcast(dt.uint8), T.wc[:, :], [], [t("wq")])
+    dma("y", "dw", T.wp[:, 0:512], T.ws[:, :], [], [t("wp")])
+    dma("y", "dv", T.vb[:, :], T.v[:, :], [], [t("vb")])
+
+    iota(t("pI", 0, 1), [[0, 1]], 0, 1)
+    iota(t("uI"), [[16, 8]])
+    iota(f("t16"), [[0, 18], [1, 16]])
+    iota(f("q16", 0, 9), [[16, 9]])
+    for i, base in enumerate((72, 216, 1, 145)):
+        iota(f("cAD", 36 * i, 36 * i + 36), [[2, 36]], base)
+    iota(f("t2"), [[0, 40], [1, 2]])
+    iota(f("t8"), [[0, 10], [1, 8]])
+    for n in ("W1", "W2"):
+        iota(f(n), [[1, 288]])
+    iota(f("J"), [[1, 80]])
+    iota(f("q32", 0, 36), [[32, 36]])
+    iota(f("t4"), [[0, 72], [1, 4]])
+    for n in ("W3", "W4"):
+        iota(f(n), [[1, 288]])
+    partner = [T.cores[rank ^ m] for m in MASKS]
+    arrives("lr0", send(partner[0], "lr0", t("lk0"), t("kld"), [t("kld")]), [t("lk0")])
+
+    def pcol(i):
+        return t("pF", i, i + 1)
+
+    cp(t("uo"), t("uI"))
+    ts(t("pI", 1, 2), t("pI", 0, 1), 15, A.bitwise_and)
+    ts(t("pI", 2, 3), t("pI", 0, 1), 3, A.bitwise_and)
+    ts(t("pI", 3, 4), t("pI", 0, 1), 15, A.bitwise_and, 2, A.arith_shift_right)
+    ts(t("pI", 4, 5), t("pI", 0, 1), 15, A.bitwise_and, 3, A.arith_shift_right)
+    ts(t("pI", 5, 6), t("pI", 0, 1), 15, A.bitwise_and, 1, A.arith_shift_right)
+    ts(t("pI", 6, 7), t("pI", 0, 1), 2, A.arith_shift_right, 1, A.bitwise_and)
+    ts(t("pI", 7, 8), t("pI", 0, 1), 1, A.bitwise_and)
+    cp(t("pF", 0, 8), t("pI"))
+    P16, P4, I4, I8, I2, PAR4, PAR2 = [pcol(i) for i in range(1, 8)]
+    equal(f("M16n"), f("t16"), P16, f("n4w"))
+    act(f("sgM", 0, 72), f("M16n", 0, 72))
+    act(f("sgM", 72, 144), f("M16n", 72, 144), -1.0)
+    ts(f("m16z"), f("t16"), 0.0, A.is_gt)
+    ts(f("cT", 0, 9), f("q16", 0, 9), P16, A.add)
+    ts(f("tA", 0, 9), f("cT", 0, 9), 36.0, A.is_ge, 72.0, A.mult)
+    ts(f("tB", 0, 9), f("cT", 0, 9), 108.0, A.is_ge, 72.0, A.mult)
+    ts(f("tC", 0, 9), f("cT", 0, 9), 72.0, A.is_ge, 287.0, A.mult)
+    ts(f("tD", 0, 9), f("cT", 0, 9), 2.0, A.mult, 72.0, A.add)
+    tt(f("tA", 0, 9), f("tA", 0, 9), f("tB", 0, 9), A.add)
+    tt(f("tD", 0, 9), f("tD", 0, 9), f("tC", 0, 9), A.subtract)
+    ts(f("sgT", 0, 9), f("cT", 0, 9), 72.0, A.is_ge, -2.0, A.mult)
+    ts(f("sgT", 0, 9), f("sgT", 0, 9), 1.0, A.add)
+    tt(f("tcAD", 0, 9), f("tA", 0, 9), f("tD", 0, 9), A.add)
+    tt(f("tcBC", 0, 9), f("tcAD", 0, 9), f("sgT", 0, 9), A.add)
+    run("v", lambda: g.vector.memset(T.one[:, 0:512], 1.0), [], [t("one")])
+    for e in range(4):
+        run("q", lambda: g.affine_select(T.et[:, 512 * e:512 * e + 512], T.one[:, 0:512], [[-1, 512]], A.is_equal, 0.0, e, 4),
+            [t("one")], [t("et", 512 * e, 512 * e + 512)])
+    cp(t("kt0"), t("kli"))
+    for e in range(4):
+        ts(t("k4t", 20 * e, 20 * e + 18), t("kli"), 4, A.mult, e, A.add)
+    quant(t("uq"), t("us"), t("ub"))
+    run("v", lambda: g.vector.tensor_copy(T.ur[:, 0:128].bitcast(dt.uint32), T.uq[:, 0:128].bitcast(dt.uint32).indirect(T.uo[:, 0:8])),
+        [t("uq"), t("uo")], [t("ur")])
+    run("s", lambda: g.scalar.activation(T.urs[:, 0:128], T.us[:, 0:128].indirect(T.uo[:, 0:8]), COPY), [t("us"), t("uo")], [t("urs")])
+    equal(f("M2"), f("t2"), I8, f("n4s", 0, 80))
+    equal(f("M8"), f("t8"), I2, f("n4s", 80, 160))
+
+    def state(r, h):
+        quant(t("xq%d" % r, 144 * h, 144 * h + 144), t("xs%d" % r, 144 * h, 144 * h + 144), t("X%d" % r, 576 * h, 576 * h + 576))
+        if r < 3:
+            mm(bank(2 + h, 144), t("ur"), t("urs"), t("xq%d" % r, 144 * h, 144 * h + 144), t("xs%d" % r, 144 * h, 144 * h + 144))
+
+    state(0, 0)
+    state(0, 1)
+
+    def constants1():
+        ts(f("M16n"), f("M16n"), -1.0, A.add, 4096.0, A.mult)
+        ts(f("d16"), f("m16z"), 16384.0, A.mult, -8192.0, A.add)
+
+    def constants2():
+        ts(f("m4z"), f("t4"), 0.0, A.is_gt)
+        for i in range(4):
+            ts(pcol(16 + i), I4, float(i), A.is_equal, 4.0, A.mult)
+        for i in range(2):
+            ts(pcol(20 + i), I8, float(i), A.is_equal)
+        ts(pcol(8), I4, 8.0, A.mult, P4, A.add)
+        ts(pcol(9), PAR4, -2.0, A.mult, 1.0, A.add)
+        ts(pcol(10), PAR2, -2.0, A.mult, 1.0, A.add)
+        ts(pcol(11), I4, 3.0, A.is_equal, 4.0, A.mult)
+        ts(pcol(12), P16, 15.0, A.is_equal)
+        ts(pcol(13), I4, 0.0, A.is_equal)
+        ts(pcol(14), P16, 0.0, A.is_equal)
+        ts(f("b1", 0, 36), f("q32", 0, 36), pcol(8), A.add)
+        ts(f("b2", 0, 36), f("b1", 0, 36), 4.0, A.add)
+        for jm, m, z in (("JM2", "M2", 13), ("JM8", "M8", 14)):
+            ts(f(jm), f("J"), 1.0, A.add)
+            tt(f(jm), f(jm), f(m), A.mult)
+            ts(f(jm), f(jm), -1.0, A.add)
+            tt(f(jm, 0, 1), f(jm, 0, 1), pcol(z), A.subtract)
+
+    def constants3():
+        ts(f("tb", 0, 9), f("cT", 0, 9), 2.0, A.mult)
+        ts(f("tb", 9, 18), f("cT", 0, 9), 2.0, A.mult, 1.0, A.add)
+        ts(f("M4n"), f("t4"), I4, A.is_equal)
+        ts(f("d4"), f("m4z"), 16384.0, A.mult, -8192.0, A.add)
+        ts(f("M4n"), f("M4n"), -1.0, A.add, 4096.0, A.mult)
+        ts(t("ki", 0, 18), t("kli"), 15, A.bitwise_and)
+        ts(t("ki", 18, 36), t("kli"), 4, A.arith_shift_right)
+        ts(t("ki", 0, 18), t("ki", 0, 18), 18, A.mult)
+        tt(t("ki", 36, 54), t("ki", 0, 18), t("ki", 18, 36), A.add)
+        cp(t("ks"), t("ki", 36, 54))
+
+    def table(out, src, n, step=16):
+        cp(out, (src[0], src[1] + step - 1, src[1] + n, step))
+
+    for r in range(3):
+        X, XK, XC, Z, H, B, kt = ["%s%d" % (n, r) for n in ("X", "XK", "XC", "Z", "H", "B", "kt")]
+        zq, zs, hq, hs, lq, ls, nt, nf, kk = ["%s%d" % (n, r) for n in ("zq", "zs", "hq", "hs", "lq", "ls", "nt", "nf", "kk")]
+        if r == 0:
+            constants1()
+        for h in range(2):
+            ts(f("bits", 144 * h, 144 * h + 144), bank(2 + h, 144), 0.0, A.is_gt)
+        actg(f("fl"), f("bits"), t(kt, 0, 9))
+
+        def half_of_xk(h):
+            if r == 0:
+                for e in (2 * h, 2 * h + 1):
+                    actg(t(XK, e, 1152, 4), t(X), t("k4t", 20 * e, 20 * e + 18), 0.5)
+            else:
+                actg(t(XK, 576 * h, 576 * h + 576), t(X), t("nt%d" % (r - 1), 36 * h, 36 * h + 36), 0.5)
+
+        half_of_xk(0)
+        gop(f("w"), f("bits"), t(kt, 0, 9), f("sgM"), A.mult)
+        scan(f("sc"), f("m16z", 0, 144), f("w"), A.mult, A.add)
+        sd = f("sc", 15, 144, 16)
+        tt(f("AD", 0, 9), f("tcAD", 0, 9), sd, A.add)
+        tt(f("BC", 0, 9), f("tcBC", 0, 9), sd, A.subtract)
+        cp(t("oAD", 0, 9), f("AD", 0, 9))
+        tt(f("W1", 72, 144), f("cAD", 0, 72), f("fl", 0, 72), A.add)
+        tt(f("W1", 144, 216), f("cAD", 72, 144), f("fl", 72, 144), A.subtract)
+        cp(t("oBC", 0, 9), f("BC", 0, 9))
+        gat(f("W2", 72, 216), f("W1"), t("oAD", 0, 9))
+        ts(t("oRi", 0, 5), f("BC", 0, 5), -72.0, A.add, 0.0, A.max)
+        gat(f("W3", 72, 216), f("W2"), t("oAD", 0, 9))
+        if r == 0:
+            constants2()
+        gop(f("tw", 0, 16), f("W3"), t("oAD", 0, 1), f("M16n", 0, 16), A.add)
+        gop(f("tw", 16, 32), f("W3"), t("oAD", 8, 9), f("M16n", 0, 16), A.add)
+        for i in range(4):
+            acts(f("fM4", i, 144, 4), f("fl", i, 144, 4), pcol(16 + i))
+        for i in range(2):
+            acts(f("fM2", i, 72, 2), f("fl", i, 72, 2), pcol(20 + i))
+        actg(f("W4", 72, 216), f("W3"), t("oAD", 0, 9))
+        half_of_xk(1)
+        scan(f("ts"), f("d16", 0, 32), f("tw"), A.min, A.max)
+        cp(t("o4", 0, 4, 2), f("ts", 15, 32, 16))
+        scan(f("fS4"), f("m4z", 0, 144), f("fM4"), A.mult, A.add)
+        gat(f("tm", 0, 16), f("W4"), t("o4", 0, 1))
+        gat(f("tm", 16, 32), f("W4"), t("o4", 2, 3))
+        cp(f("W4", 72, 88), f("tm", 0, 16))
+        cp(f("W4", 200, 216), f("tm", 16, 32))
+        gop(f("Vw"), f("W4"), t("oBC", 0, 5), f("M16n", 0, 80), A.add)
+        actg(f("Vb"), f("W4"), t("oBC", 4, 9))
+        scan(f("Vs"), f("d16", 0, 80), f("Vw"), A.min, A.max)
+        gop(f("Rw"), f("W4"), t("oRi", 0, 5), f("M16n", 0, 80), A.add)
+        ts(t("oVC", 0, 5), f("Vs", 15, 80, 16), -208.0, A.add, 8.0, A.max)
+        scan(f("Rs"), f("d16", 0, 80), f("Rw"), A.min, A.max)
+        gop(f("Pw"), f("Vb"), t("oVC", 0, 5), f("M16n", 0, 80), A.add)
+        actg(f("F0"), f("Vb"), t("oVC", 0, 5))
+        scan(f("Ps"), f("d16", 0, 80), f("Pw"), A.min, A.max)
+        ts(t("oR", 0, 5), f("Rs", 15, 80, 16), 71.0, A.min)
+        table(t("oP0", 0, 5), f("Ps"), 80)
+        tt(f("dj", 0, 36), f("fM2", 0, 72, 2), f("fM2", 1, 72, 2), A.add)
+        low = f("J")
+        for i in range(4):
+            o = t("oP%d" % i, 0, 5)
+            Fi, Gi, la, lb = f("F%d" % (i % 3)), f("G%d" % (i % 3)), f("l%d" % (2 * i)), f("l%d" % (2 * i + 1))
+            if i < 3:
+                gat(Gi, Fi, o)
+            if i == 0:
+                tt(la, Fi, low, A.min)
+            else:
+                gop(la, low, o, f("lc"), A.min)
+            if i < 3:
+                gop(f("Gw"), Gi, o, f("M16n", 0, 80), A.add)
+                gop(lb, la, o, low, A.min)
+                if i < 2:
+                    actg(f("F%d" % (i + 1)), Gi, o)
+                act(f("lc"), lb)
+                if i == 1:
+                    act(t(XC, 0, 576), t(XK, 0, 576))
+                if i == 2:
+                    act(t(XC, 576, 1152), t(XK, 576, 1152))
+                if i == 0:
+                    table(f("dn", 0, 36), f("fS4"), 144, 4)
+                elif i == 1:
+                    ts(f("s1", 0, 36), f("dn", 0, 36), -2.0, A.mult, 4.0, A.add)
+                else:
+                    tt(f("c1", 0, 36), f("b1", 0, 36), f("dn", 0, 36), A.add)
+                scan(f("Gs"), f("d16", 0, 80), f("Gw"), A.min, A.max)
+                if i == 0:
+                    tt(f("dn", 35, 36), f("dn", 35, 36), pcol(11), A.max)
+                elif i == 1:
+                    tt(f("dh", 0, 36), f("s1", 0, 36), f("fs", 0, 36), A.mult)
+                else:
+                    tt(f("c2", 0, 36), f("b2", 0, 36), f("dn", 0, 36), A.subtract)
+                table(t("oP%d" % (i + 1), 0, 5), f("Gs"), 80)
+                if i == 0:
+                    ts(f("fs", 0, 36), f("dj", 0, 36), pcol(9), A.mult, PAR4, A.add)
+            else:
+                gop(lb, la, o, f("lc"), A.min)
+            low = lb
+        gop(f("b"), low, t("oR", 0, 5), f("J"), A.not_equal)
+        tt(f("a", 0, 72), (low[0], low[1], low[1] + 72, 1), f("JM2", 0, 72), A.is_equal)
+        tt(f("cd", 0, 72), f("a", 0, 72), f("b", 0, 72), A.mult)
+        tt(f("dc", 0, 36), f("cd", 0, 72, 2), f("cd", 1, 72, 2), A.add)
+        tt(f("dy", 0, 36), f("dc", 0, 36), f("dh", 0, 36), A.mult)
+        tt(f("tab", 0, 36), f("c1", 0, 36), f("dy", 0, 36), A.add)
+        tt(f("tab", 36, 72), f("c2", 0, 36), f("dy", 0, 36), A.subtract)
+        cp(t("tt4", 0, 36), f("tab", 0, 36))
+        cp(t("tt4", 36, 72), f("tab", 36, 72))
+        for h in range(2):
+            gop(t(Z, 576 * h, 576 * h + 576), t(XK), t("tt4", 36 * h, 36 * h + 36), t(XC, 576 * h, 576 * h + 576), A.add)
+            quant(t(zq, 144 * h, 144 * h + 144), t(zs, 144 * h, 144 * h + 144), t(Z, 576 * h, 576 * h + 576))
+            for b in range(4):
+                mm(bank(4 + 4 * h + b, 144), t("wq", 128 * b, 128 * b + 128), t("wp", 128 * b, 128 * b + 128),
+                   t(zq, 144 * h, 144 * h + 144), t(zs, 144 * h, 144 * h + 144))
+                if h == 0:
+                    act(t(H, b, 576, 4), bank(4 + b, 144), 0.03125)
+        quant(t(hq, 0, 144), t(hs, 0, 144), t(H, 0, 576))
+        dst = partner[r]
+        n = send(dst, "ha%d" % r, t(lq, 0, C1), t(hq, 0, C1), [t(hq, 0, C1)], True)
+        n += send(dst, "ha%d" % r, t(ls, 0, C1), t(hs, 0, C1), [t(hs, 0, C1)])
+        def second(b):
+            k = bank(8 + b, 144)
+            return (k[0], k[1], k[1] + C2, 1), (k[0], k[1] + C2, k[1] + 144, 1)
+        for b in range(4):
+            act(t(H, 576 + b, 896, 4), second(b)[0], 0.03125)
+        if r == 0:
+            ts(f("m8z"), f("t8"), 0.0, A.is_gt)
+        tt(f("fM8", 0, 72), f("fl", 0, 72), f("M8", 0, 72), A.mult)
+        tt(f("a8", 0, 72), (low[0], low[1], low[1] + 72, 1), f("JM8", 0, 72), A.is_equal)
+        tt(f("f18", 0, 9), sd, f("sgT", 0, 9), A.mult)
+        scan(f("fS8", 0, 72), f("m8z", 0, 72), f("fM8", 0, 72), A.mult, A.add)
+        tt(f("f18", 8, 9), f("f18", 8, 9), pcol(12), A.max)
+        ts(f("fs18", 0, 9), f("fS8", 7, 72, 8), pcol(10), A.mult, PAR2, A.add)
+        quant(t(hq, C1, C1 + 128), t(hs, C1, C1 + 128), t(H, 4 * (E - 128), 4 * E))
+        m = send(dst, "hb%d" % r, t(lq, C1, E), t(hq, C1 + 128 - C2, C1 + 128), [t(hq, C1, C1 + 128)], True)
+        m += send(dst, "hb%d" % r, t(ls, C1, E), t(hs, C1 + 128 - C2, C1 + 128), [t(hs, C1, C1 + 128)])
+        arrives("ha%d" % r, n, [t(lq, 0, C1), t(ls, 0, C1)])
+        arrives("hb%d" % r, m, [t(lq, C1, E), t(ls, C1, E)])
+        for b in range(4):
+            act(t(B, 4 * E + b, 4 * C, 4), second(b)[1], 0.03125)
+        if r == 0:
+            constants3()
+        kf, lk = "kf%d" % r, "lk%d" % r
+        for i in range(16):
+            dma("y", "df%d" % r, T[kf][i:128:16, :], T[lk][:, :], [t(lk)], [(kf, i, C, 16)])
+        tt(f("c8", 0, 72), f("a8", 0, 72), f("b", 0, 72), A.mult)
+        ts(f("s18", 0, 9), f("f18", 0, 9), -2.0, A.mult, 1.0, A.add)
+        scan(f("cS8", 0, 72), f("m8z", 0, 72), f("c8", 0, 72), A.mult, A.add)
+        tt(f("h18", 0, 9), f("fs18", 0, 9), f("s18", 0, 9), A.mult)
+        tt(f("dy18", 0, 9), f("h18", 0, 9), f("cS8", 7, 72, 8), A.mult)
+        tt(f("f18", 0, 9), f("f18", 0, 9), f("dy18", 0, 9), A.add)
+        tt(f("tab18", 0, 9), f("tb", 0, 9), f("f18", 0, 9), A.add)
+        tt(f("tab18", 9, 18), f("tb", 9, 18), f("f18", 0, 9), A.subtract)
+        cp(t("tt18"), f("tab18", 0, 18))
+        if r == 0:
+            gat(t(kk), t(kf), t("ks"))
+        else:
+            actg(t(kk), t(kf), t(kt))
+        gop(f("n4w"), t(kk), t("tt18"), f("M4n"), A.add)
+        actg(t(nf), t(kk), t("tt18"))
+        scan(f("n4s"), f("d4"), f("n4w"), A.min, A.max)
+        if r < 2:
+            gop(f("n16w"), t(kk), t("tt18"), f("M16n"), A.add)
+        ts(t(nt), f("n4s", 3, 288, 4), 4.0, A.mult, P4, A.add)
+        if r < 2:
+            scan(f("n16s"), f("d16"), f("n16w"), A.min, A.max)
+            table(t("kt%d" % (r + 1)), f("n16s"), 288)
+            nd = "nd%d" % (r + 1)
+            dma("y", "dn%d" % (r + 1), T[nd][:, :], T[nf][0:128:16, :], [t(nf)], [t(nd)])
+            lr = "lr%d" % (r + 1)
+            arrives(lr, send(partner[r + 1], lr, t("lk%d" % (r + 1)), t(nd), [t(nd)]), [t("lk%d" % (r + 1))])
+        else:
+            dma("y", "dout", T.kp[:, :], T[nf][0:128:16, :], [t(nf)], [])
+        if r == 0:
+            quant(t("eq"), t("es"), t("et"))
+            quant(t("vq"), t("vs"), t("vb"))
+        for c0, c1, new, at in ((0, C1, 0, 12), (E - 128, E, 128 - C2, 16)):
+            for b in range(4):
+                mm(bank(at + b, c1 - c0), t("eq", 128 * b, 128 * b + 128), t("es", 128 * b, 128 * b + 128), t(lq, c0, c1), t(ls, c0, c1))
+                k = bank(at + b, c1 - c0)
+                k = (k[0], k[1] + new, k[2], 1)
+                o = t(B, 4 * (c0 + new) + b, 4 * c1, 4)
+                act(o, k)
+        Xn = "X%d" % (r + 1)
+        for h in range(2):
+            gop(t(Xn, 576 * h, 576 * h + 576), t(B), t(nt, 36 * h, 36 * h + 36), t(X, 576 * h, 576 * h + 576), A.add)
+            state(r + 1, h)
+            if r == 2:
+                q, s = "xq3", "xs3"
+                a, b = 144 * h, 144 * h + 144
+                mm(bank(2 + h, 144), t("vq"), t("vs"), t(q, a, b), t(s, a, b))
+                dma("y", "dout", T.oc[:, 4 * a:4 * b], T[q][:, a:b].bitcast(dt.uint8), [t(q, a, b)], [])
+                for i in range(4):
+                    dma("y", "dout", T.osc[4 * i:4 * i + 4, a:b], T[s][32 * i:32 * i + 4, a:b], [t(s, a, b)], [])
+                act(t("ysb", a, b), bank(2 + h, 144))
+                dma("s", "dout", T.y[:, a:b], T.ysb[:, a:b], [t("ysb", a, b)], [])
+    need("y", "dout", total["dout"])
+    need("q", "sent", total["sent"])
+    for sem in ("v", "s", "p", "q"):
+        need("y", sem, total[sem])

@@ -3,7 +3,7 @@ from concourse.mybir import dt, AluOpType, AxisListType, ActivationFunctionType
 
 C, HALF, E = 288, 144, 224
 MASKS = [4, 1, 2]
-C1 = 144
+C1 = 128
 C2 = E - C1
 F4 = "float8_e4m3fn_x4"
 
@@ -41,8 +41,8 @@ for _i in range(3):
     SCRATCH["Z%d" % _i] = ("sbuf", [128, 4 * C], "bfloat16")
     SCRATCH["H%d" % _i] = ("sbuf", [128, 4 * E], "bfloat16")
     SCRATCH["B%d" % _i] = ("sbuf", [128, 4 * C], "bfloat16")
-    SCRATCH["zq%d" % _i] = ("sbuf", [128, C], F4)
-    SCRATCH["zs%d" % _i] = ("sbuf", [128, C], "uint8")
+    SCRATCH["zq%d" % _i] = ("sbuf", [128, 384], F4)
+    SCRATCH["zs%d" % _i] = ("sbuf", [128, 384], "uint8")
     SCRATCH["hq%d" % _i] = ("sbuf", [128, C1 + 128], F4)
     SCRATCH["hs%d" % _i] = ("sbuf", [128, C1 + 128], "uint8")
     SCRATCH["lq%d" % _i] = ("sbuf", [128, E], F4)
@@ -51,24 +51,27 @@ for _i in range(3):
     SCRATCH["nf%d" % _i] = ("sbuf", [128, C], "float32")
     SCRATCH["kk%d" % _i] = ("sbuf", [128, C], "float32")
 _ROWS = {
-    "t16": 288, "t4": 288, "t8": 80, "t2": 80, "J": 80, "q16": 16, "q32": 40,
-    "W1": 288, "W2": 288, "W3": 288, "W4": 288, "cAD": 144, "sgM": 144, "M16n": 288, "M4n": 288, "M2": 80, "M8": 80,
-    "m16z": 288, "m8z": 80, "m4z": 288, "d16": 288, "d4": 288, "JM2": 80, "JM8": 80,
-    "cT": 16, "tA": 16, "tB": 16, "tC": 16, "tD": 16, "tcAD": 16, "tcBC": 16, "sgT": 16, "tb": 24, "b1": 40, "b2": 40,
-    "bits": 288, "fl": 144, "w": 144, "sc": 144, "AD": 16, "BC": 16, "tw": 32, "ts": 32, "tm": 32,
-    "Vw": 80, "Vs": 80, "Vb": 80, "Pw": 80, "Ps": 80, "F0": 80, "F1": 80, "F2": 80, "G0": 80, "G1": 80, "G2": 80,
-    "Gw": 80, "Gs": 80, "l0": 80, "l1": 80, "l2": 80, "l3": 80, "l4": 80, "l5": 80, "l6": 80, "l7": 80, "lc": 80,
-    "Rw": 80, "Rs": 80, "fM4": 144, "fS4": 144, "fM2": 80, "dn": 40, "dj": 40, "s1": 40, "fs": 40, "dh": 40, "c1": 40, "c2": 40,
-    "a": 80, "b": 80, "cd": 80, "dc": 40, "dy": 40, "tab": 72,
-    "fM8": 80, "fS8": 80, "a8": 80, "c8": 80, "cS8": 80, "f18": 16, "s18": 16, "fs18": 16, "h18": 16, "dy18": 16, "tab18": 24,
-    "n4w": 288, "n4s": 288, "n16w": 288, "n16s": 288,
+    "t16": 288, "t4": 288, "t8": 80, "t2": 80, "t32": 288, "J1": 80, "J2": 80, "q16": 16, "q32": 40, "m144": 288, "tmp": 288,
+    "W1": 288, "W2": 288, "W3": 288, "W4": 288, "W5": 288, "cAD": 144, "sgM": 144, "M16n": 288, "M4n": 288, "M2": 80, "M8": 80,
+    "m8z": 80, "d16": 80, "JM2": 80, "JM8": 80,
+    "cT": 16, "tA": 16, "tB": 16, "tC": 16, "tD": 16, "tcAD": 16, "tcBC": 16, "sgT": 16, "tb": 16, "cc18": 16,
+    "b1": 40, "cc4": 40, "bits": 288, "fl": 144, "BC": 16, "tw": 32, "ts": 32,
+    "Vw": 80, "Vs": 80, "Vb": 80, "F0": 80, "F1": 80, "F2": 80, "G0": 80, "G1": 80, "G2": 80,
+    "l0": 80, "l1": 80, "l2": 80, "l3": 80, "l4": 80, "l5": 80, "l6": 80, "l7": 80, "lc": 80,
+    "fM2": 80, "dj": 40, "s1": 40, "fs": 40, "a": 80, "b": 80, "x4": 144, "z4": 144, "xs4": 144, "tab2": 40,
+    "fM8": 80, "fS8": 80, "a8": 80, "f18": 16, "s18": 16, "fs18": 16, "x8": 144, "z8": 144, "xs8": 144, "up": 16,
+}
+_ROWS2 = {
+    "x2": 288, "z2": 288, "xs2": 288, "n4w": 288, "n4s": 288, "n16w": 288, "n16s": 288, "d4": 288, "d16b": 288,
+    "Pw": 80, "Ps": 80, "Rw": 80, "Rs": 80, "Gw": 80, "Gs": 80, "fM4": 144, "fS4": 144, "m4z": 144,
 }
 OFF = {}
-_n = 0
-for _k, _v in _ROWS.items():
-    OFF[_k] = _n
-    _n += (_v + 7) // 8 * 8
-SCRATCH["F"] = ("sbuf", [128, _n], "float32")
+for _b, _t, _d in (("F", _ROWS, "float32"), ("G", _ROWS2, "bfloat16")):
+    _n = 0
+    for _k, _v in _t.items():
+        OFF[_k] = (_b, _n, _v)
+        _n += (_v + 15) // 16 * 16
+    SCRATCH[_b] = ("sbuf", [128, _n], _d)
 
 SEMAPHORES = ["v", "s", "p", "q", "sent", "dx0", "dx1", "dk", "du", "dw", "dv", "dkl", "dn1", "dn2", "df0", "df1", "df2", "dout",
               "lr0", "lr1", "lr2", "ha0", "ha1", "ha2", "hb0", "hb1", "hb2"]
@@ -79,13 +82,13 @@ def rank_program(g, core, T, topo):
     if rank is None:
         return
     A = AluOpType
-    COPY = ActivationFunctionType.Copy
+    COPY, IDENT, SIGN = ActivationFunctionType.Copy, ActivationFunctionType.Identity, ActivationFunctionType.Sign
     queue = {"v": g.vector, "s": g.scalar, "p": g.tensor, "q": g, "y": g.sync}
     total, known, log = {}, {}, {}
 
     def f(name, a=0, b=None, step=1):
         o = OFF[name]
-        return ("F", o + a, o + (_ROWS[name] if b is None else b), step)
+        return (o[0], o[1] + a, o[1] + (o[2] if b is None else b), step)
 
     def t(name, a=0, b=None, step=1):
         return (name, a, SCRATCH[name][1][1] if b is None else b, step)
@@ -179,8 +182,14 @@ def rank_program(g, core, T, topo):
         actf(tmp, a, ActivationFunctionType.Abs, -1.0, col)
         actf(out, tmp, ActivationFunctionType.Relu, -1.0, 1.0)
 
-    def actg(out, win, off, scale=1.0):
-        run("s", lambda: g.scalar.activation(ap(out), ind(win, off), COPY, scale=scale), [win, off], [out])
+    def actg(out, win, off, scale=1.0, bias=None):
+        if bias is None:
+            run("s", lambda: g.scalar.activation(ap(out), ind(win, off), COPY, scale=scale), [win, off], [out])
+        else:
+            run("s", lambda: g.scalar.activation(ap(out), ind(win, off), IDENT, bias=bias), [win, off], [out])
+
+    def fill(out, c):
+        run("v", lambda: g.vector.memset(ap(out), c), [], [out])
 
     def quant(q, s, a):
         run("v", lambda: g.vector.quantize_mx(ap(q), ap(s), ap(a)), [a], [q, s])
@@ -218,6 +227,7 @@ def rank_program(g, core, T, topo):
     dma("s", "du", T.ub[:, :], T.u[:, :], [], [t("ub")])
     dma("y", "dx1", T.X0[:, 576:1152], T.x[:, 576:1152], [], [t("X0", 576, 1152)])
     dma("y", "dkl", T.kld[:, :], T.kl[:, :], [], [t("kld")])
+    need("y", "dx1", 16)
     dma("y", "dw", T.wq[:, 0:512].bitcast(dt.uint8), T.wc[:, :], [], [t("wq")])
     dma("y", "dw", T.wp[:, 0:512], T.ws[:, :], [], [t("wp")])
     dma("y", "dv", T.vb[:, :], T.v[:, :], [], [t("vb")])
@@ -226,17 +236,15 @@ def rank_program(g, core, T, topo):
     iota(t("uI"), [[16, 8]])
     iota(f("t16"), [[0, 18], [1, 16]])
     iota(f("q16", 0, 9), [[16, 9]])
-    for i, base in enumerate((72, 216, 1, 145)):
-        iota(f("cAD", 36 * i, 36 * i + 36), [[2, 36]], base)
+    iota(f("t32"), [[0, 9], [1, 32]])
     iota(f("t2"), [[0, 40], [1, 2]])
     iota(f("t8"), [[0, 10], [1, 8]])
-    for n in ("W1", "W2"):
-        iota(f(n), [[1, 288]])
-    iota(f("J"), [[1, 80]])
+    iota(f("J1"), [[1, 80]], 1)
     iota(f("q32", 0, 36), [[32, 36]])
+    for i, base in enumerate((72, 216, 1, 145)):
+        iota(f("cAD", 36 * i, 36 * i + 36), [[2, 36]], base)
+    iota(f("W1"), [[1, 288]])
     iota(f("t4"), [[0, 72], [1, 4]])
-    for n in ("W3", "W4"):
-        iota(f(n), [[1, 288]])
     partner = [T.cores[rank ^ m] for m in MASKS]
     arrives("lr0", send(partner[0], "lr0", t("lk0"), t("kld"), [t("kld")]), [t("lk0")])
 
@@ -253,10 +261,11 @@ def rank_program(g, core, T, topo):
     ts(t("pI", 7, 8), t("pI", 0, 1), 1, A.bitwise_and)
     cp(t("pF", 0, 8), t("pI"))
     P16, P4, I4, I8, I2, PAR4, PAR2 = [pcol(i) for i in range(1, 8)]
-    equal(f("M16n"), f("t16"), P16, f("n4w"))
+    equal(f("M16n"), f("t16"), P16, f("tmp"))
     act(f("sgM", 0, 72), f("M16n", 0, 72))
     act(f("sgM", 72, 144), f("M16n", 72, 144), -1.0)
-    ts(f("m16z"), f("t16"), 0.0, A.is_gt)
+    actf(f("m144"), f("t16"), IDENT, 0.0, -144.0)
+    fill(f("x2"), 0.0)
     ts(f("cT", 0, 9), f("q16", 0, 9), P16, A.add)
     ts(f("tA", 0, 9), f("cT", 0, 9), 36.0, A.is_ge, 72.0, A.mult)
     ts(f("tB", 0, 9), f("cT", 0, 9), 108.0, A.is_ge, 72.0, A.mult)
@@ -268,6 +277,7 @@ def rank_program(g, core, T, topo):
     ts(f("sgT", 0, 9), f("sgT", 0, 9), 1.0, A.add)
     tt(f("tcAD", 0, 9), f("tA", 0, 9), f("tD", 0, 9), A.add)
     tt(f("tcBC", 0, 9), f("tcAD", 0, 9), f("sgT", 0, 9), A.add)
+    ts(f("x2", 31, 288, 32), f("tcAD", 0, 9), -144.0, A.add)
     run("v", lambda: g.vector.memset(T.one[:, 0:512], 1.0), [], [t("one")])
     for e in range(4):
         run("q", lambda: g.affine_select(T.et[:, 512 * e:512 * e + 512], T.one[:, 0:512], [[-1, 512]], A.is_equal, 0.0, e, 4),
@@ -275,12 +285,23 @@ def rank_program(g, core, T, topo):
     cp(t("kt0"), t("kli"))
     for e in range(4):
         ts(t("k4t", 20 * e, 20 * e + 18), t("kli"), 4, A.mult, e, A.add)
+    actf(f("z2"), f("t32"), SIGN, 1.0, 0.0)
+    equal(f("M2"), f("t2"), I8, f("tmp", 0, 80))
+    equal(f("M8"), f("t8"), I2, f("tmp", 80, 160))
+    act(f("J2"), f("J1"))
+    fill(f("x4"), 0.0)
+    fill(f("x8"), 0.0)
     quant(t("uq"), t("us"), t("ub"))
     run("v", lambda: g.vector.tensor_copy(T.ur[:, 0:128].bitcast(dt.uint32), T.uq[:, 0:128].bitcast(dt.uint32).indirect(T.uo[:, 0:8])),
         [t("uq"), t("uo")], [t("ur")])
     run("s", lambda: g.scalar.activation(T.urs[:, 0:128], T.us[:, 0:128].indirect(T.uo[:, 0:8]), COPY), [t("us"), t("uo")], [t("urs")])
-    equal(f("M2"), f("t2"), I8, f("n4s", 0, 80))
-    equal(f("M8"), f("t8"), I2, f("n4s", 80, 160))
+
+    def ends(n):
+        act(f(n, 0, 72), f("W1", 0, 72))
+        act(f(n, 216, 288), f("W1", 216, 288))
+
+    ends("W2")
+    ends("W3")
 
     def state(r, h):
         quant(t("xq%d" % r, 144 * h, 144 * h + 144), t("xs%d" % r, 144 * h, 144 * h + 144), t("X%d" % r, 576 * h, 576 * h + 576))
@@ -292,40 +313,35 @@ def rank_program(g, core, T, topo):
 
     def constants1():
         ts(f("M16n"), f("M16n"), -1.0, A.add, 4096.0, A.mult)
-        ts(f("d16"), f("m16z"), 16384.0, A.mult, -8192.0, A.add)
+        ts(f("d16"), f("t16", 0, 80), 0.0, A.is_gt, 16384.0, A.mult)
+        ts(f("d16"), f("d16"), -8192.0, A.add)
+        cp(f("d16b", 0, 80), f("d16"))
 
     def constants2():
-        ts(f("m4z"), f("t4"), 0.0, A.is_gt)
-        for i in range(4):
-            ts(pcol(16 + i), I4, float(i), A.is_equal, 4.0, A.mult)
-        for i in range(2):
-            ts(pcol(20 + i), I8, float(i), A.is_equal)
-        ts(pcol(8), I4, 8.0, A.mult, P4, A.add)
-        ts(pcol(9), PAR4, -2.0, A.mult, 1.0, A.add)
-        ts(pcol(10), PAR2, -2.0, A.mult, 1.0, A.add)
-        ts(pcol(11), I4, 3.0, A.is_equal, 4.0, A.mult)
-        ts(pcol(12), P16, 15.0, A.is_equal)
+        ts(t("pF", 16, 20), f("t4", 0, 4), I4, A.is_equal, 4.0, A.mult)
+        ts(t("pF", 20, 22), f("t4", 0, 2), I8, A.is_equal)
+        ts(t("pF", 9, 11), t("pF", 6, 8), -2.0, A.mult, 1.0, A.add)
         ts(pcol(13), I4, 0.0, A.is_equal)
-        ts(pcol(14), P16, 0.0, A.is_equal)
-        ts(f("b1", 0, 36), f("q32", 0, 36), pcol(8), A.add)
-        ts(f("b2", 0, 36), f("b1", 0, 36), 4.0, A.add)
-        for jm, m, z in (("JM2", "M2", 13), ("JM8", "M8", 14)):
-            ts(f(jm), f("J"), 1.0, A.add)
-            tt(f(jm), f(jm), f(m), A.mult)
-            ts(f(jm), f(jm), -1.0, A.add)
-            tt(f(jm, 0, 1), f(jm, 0, 1), pcol(z), A.subtract)
+        ts(pcol(8), I4, 8.0, A.mult, P4, A.add)
+        ts(pcol(12), P16, 15.0, A.is_equal)
+        tt(f("JM2"), f("J1"), f("M2"), A.mult)
+        tt(f("JM2", 0, 1), f("JM2", 0, 1), pcol(13), A.subtract)
+        actf(f("b1", 0, 36), f("q32", 0, 36), IDENT, 1.0, pcol(8))
+        actf(f("cc4", 0, 36), f("b1", 0, 36), IDENT, 2.0, 4.0)
 
     def constants3():
-        ts(f("tb", 0, 9), f("cT", 0, 9), 2.0, A.mult)
-        ts(f("tb", 9, 18), f("cT", 0, 9), 2.0, A.mult, 1.0, A.add)
+        ts(pcol(14), P16, 0.0, A.is_equal)
+        ts(pcol(15), P4, 576.0, A.add)
+        tt(f("JM8"), f("J1"), f("M8"), A.mult)
+        tt(f("JM8", 0, 1), f("JM8", 0, 1), pcol(14), A.subtract)
+
+    def constants4():
         ts(f("M4n"), f("t4"), I4, A.is_equal)
-        ts(f("d4"), f("m4z"), 16384.0, A.mult, -8192.0, A.add)
+        ts(f("tmp"), f("t4"), 0.0, A.is_gt, 16384.0, A.mult)
         ts(f("M4n"), f("M4n"), -1.0, A.add, 4096.0, A.mult)
-        ts(t("ki", 0, 18), t("kli"), 15, A.bitwise_and)
-        ts(t("ki", 18, 36), t("kli"), 4, A.arith_shift_right)
-        ts(t("ki", 0, 18), t("ki", 0, 18), 18, A.mult)
-        tt(t("ki", 36, 54), t("ki", 0, 18), t("ki", 18, 36), A.add)
-        cp(t("ks"), t("ki", 36, 54))
+        ts(f("d4"), f("tmp"), -8192.0, A.add)
+        ts(f("tmp"), f("t16"), 0.0, A.is_gt, 16384.0, A.mult)
+        ts(f("d16b"), f("tmp"), -8192.0, A.add)
 
     def table(out, src, n, step=16):
         cp(out, (src[0], src[1] + step - 1, src[1] + n, step))
@@ -333,6 +349,9 @@ def rank_program(g, core, T, topo):
     for r in range(3):
         X, XK, XC, Z, H, B, kt = ["%s%d" % (n, r) for n in ("X", "XK", "XC", "Z", "H", "B", "kt")]
         zq, zs, hq, hs, lq, ls, nt, nf, kk = ["%s%d" % (n, r) for n in ("zq", "zs", "hq", "hs", "lq", "ls", "nt", "nf", "kk")]
+        kf, lk = "kf%d" % r, "lk%d" % r
+        for i in range(16):
+            dma("y", "df%d" % r, T[kf][i:128:16, :], T[lk][:, :], [t(lk)], [(kf, i, C, 16)])
         if r == 0:
             constants1()
         for h in range(2):
@@ -347,12 +366,16 @@ def rank_program(g, core, T, topo):
                 actg(t(XK, 576 * h, 576 * h + 576), t(X), t("nt%d" % (r - 1), 36 * h, 36 * h + 36), 0.5)
 
         half_of_xk(0)
-        gop(f("w"), f("bits"), t(kt, 0, 9), f("sgM"), A.mult)
-        scan(f("sc"), f("m16z", 0, 144), f("w"), A.mult, A.add)
-        sd = f("sc", 15, 144, 16)
-        tt(f("AD", 0, 9), f("tcAD", 0, 9), sd, A.add)
+        if r == 0:
+            ends("W4")
+            ends("W5")
+            actf(f("m4z"), f("t4", 0, 144), SIGN, 1.0, 0.0)
+            actf(f("z4"), f("t4", 0, 144), SIGN, 1.0, 0.0)
+        gop(f("x2", 0, 288, 2), f("bits"), t(kt, 0, 9), f("sgM"), A.mult)
+        scan(f("xs2"), f("z2"), f("x2"), A.mult, A.add)
+        sd = f("xs2", 30, 288, 32)
+        ts(t("oAD", 0, 9), f("xs2", 31, 288, 32), 144.0, A.add)
         tt(f("BC", 0, 9), f("tcBC", 0, 9), sd, A.subtract)
-        cp(t("oAD", 0, 9), f("AD", 0, 9))
         tt(f("W1", 72, 144), f("cAD", 0, 72), f("fl", 0, 72), A.add)
         tt(f("W1", 144, 216), f("cAD", 72, 144), f("fl", 72, 144), A.subtract)
         cp(t("oBC", 0, 9), f("BC", 0, 9))
@@ -365,37 +388,45 @@ def rank_program(g, core, T, topo):
         gop(f("tw", 16, 32), f("W3"), t("oAD", 8, 9), f("M16n", 0, 16), A.add)
         for i in range(4):
             acts(f("fM4", i, 144, 4), f("fl", i, 144, 4), pcol(16 + i))
+        act(f("fM4", 143, 144), pcol(19))
         for i in range(2):
             acts(f("fM2", i, 72, 2), f("fl", i, 72, 2), pcol(20 + i))
         actg(f("W4", 72, 216), f("W3"), t("oAD", 0, 9))
+        actg(f("W5", 72, 216), f("W3"), t("oAD", 0, 9))
+        if r == 0:
+            actf(f("z8"), f("t16", 0, 144), SIGN, 1.0, 0.0)
+            actf(f("m8z"), f("t8"), SIGN, 1.0, 0.0)
+            actf(f("tb", 0, 9), f("cT", 0, 9), IDENT, 2.0, 0.0)
+            actf(f("cc18", 0, 9), f("cT", 0, 9), IDENT, 4.0, 1.0)
         half_of_xk(1)
         scan(f("ts"), f("d16", 0, 32), f("tw"), A.min, A.max)
         cp(t("o4", 0, 4, 2), f("ts", 15, 32, 16))
-        scan(f("fS4"), f("m4z", 0, 144), f("fM4"), A.mult, A.add)
-        gat(f("tm", 0, 16), f("W4"), t("o4", 0, 1))
-        gat(f("tm", 16, 32), f("W4"), t("o4", 2, 3))
-        cp(f("W4", 72, 88), f("tm", 0, 16))
-        cp(f("W4", 200, 216), f("tm", 16, 32))
-        gop(f("Vw"), f("W4"), t("oBC", 0, 5), f("M16n", 0, 80), A.add)
-        actg(f("Vb"), f("W4"), t("oBC", 4, 9))
-        scan(f("Vs"), f("d16", 0, 80), f("Vw"), A.min, A.max)
-        gop(f("Rw"), f("W4"), t("oRi", 0, 5), f("M16n", 0, 80), A.add)
+        scan(f("fS4"), f("m4z"), f("fM4"), A.mult, A.add)
+        gat(f("W5", 72, 88), f("W4"), t("o4", 0, 1))
+        gat(f("W5", 200, 216), f("W4"), t("o4", 2, 3))
+        tt(f("dj", 0, 36), f("fM2", 0, 72, 2), f("fM2", 1, 72, 2), A.add)
+        gop(f("Vw"), f("W5"), t("oBC", 0, 5), f("M16n", 0, 80), A.add)
+        actg(f("Vb"), f("W5"), t("oBC", 4, 9))
+        ts(f("s1", 0, 36), f("fS4", 3, 144, 4), -2.0, A.mult, 4.0, A.add)
+        scan(f("Vs"), f("d16"), f("Vw"), A.min, A.max)
+        gop(f("Rw"), f("W5"), t("oRi", 0, 5), f("M16n", 0, 80), A.add)
         ts(t("oVC", 0, 5), f("Vs", 15, 80, 16), -208.0, A.add, 8.0, A.max)
-        scan(f("Rs"), f("d16", 0, 80), f("Rw"), A.min, A.max)
+        scan(f("Rs"), f("d16b", 0, 80), f("Rw"), A.min, A.max)
+        ts(f("fs", 0, 36), f("dj", 0, 36), pcol(9), A.mult, PAR4, A.add)
         gop(f("Pw"), f("Vb"), t("oVC", 0, 5), f("M16n", 0, 80), A.add)
         actg(f("F0"), f("Vb"), t("oVC", 0, 5))
-        scan(f("Ps"), f("d16", 0, 80), f("Pw"), A.min, A.max)
+        tt(f("x4", 3, 144, 4), f("b1", 0, 36), f("fS4", 3, 144, 4), A.add)
+        scan(f("Ps"), f("d16b", 0, 80), f("Pw"), A.min, A.max)
         ts(t("oR", 0, 5), f("Rs", 15, 80, 16), 71.0, A.min)
         table(t("oP0", 0, 5), f("Ps"), 80)
-        tt(f("dj", 0, 36), f("fM2", 0, 72, 2), f("fM2", 1, 72, 2), A.add)
-        low = f("J")
+        low = f("J1")
         for i in range(4):
             o = t("oP%d" % i, 0, 5)
             Fi, Gi, la, lb = f("F%d" % (i % 3)), f("G%d" % (i % 3)), f("l%d" % (2 * i)), f("l%d" % (2 * i + 1))
             if i < 3:
                 gat(Gi, Fi, o)
             if i == 0:
-                tt(la, Fi, low, A.min)
+                gop(la, low, o, f("J2"), A.min)
             else:
                 gop(la, low, o, f("lc"), A.min)
             if i < 3:
@@ -408,93 +439,84 @@ def rank_program(g, core, T, topo):
                     act(t(XC, 0, 576), t(XK, 0, 576))
                 if i == 2:
                     act(t(XC, 576, 1152), t(XK, 576, 1152))
+                scan(f("Gs"), f("d16b", 0, 80), f("Gw"), A.min, A.max)
                 if i == 0:
-                    table(f("dn", 0, 36), f("fS4"), 144, 4)
+                    tt(f("z4", 3, 144, 4), f("s1", 0, 36), f("fs", 0, 36), A.mult)
                 elif i == 1:
-                    ts(f("s1", 0, 36), f("dn", 0, 36), -2.0, A.mult, 4.0, A.add)
+                    tt(f("f18", 0, 9), sd, f("sgT", 0, 9), A.mult)
                 else:
-                    tt(f("c1", 0, 36), f("b1", 0, 36), f("dn", 0, 36), A.add)
-                scan(f("Gs"), f("d16", 0, 80), f("Gw"), A.min, A.max)
-                if i == 0:
-                    tt(f("dn", 35, 36), f("dn", 35, 36), pcol(11), A.max)
-                elif i == 1:
-                    tt(f("dh", 0, 36), f("s1", 0, 36), f("fs", 0, 36), A.mult)
-                else:
-                    tt(f("c2", 0, 36), f("b2", 0, 36), f("dn", 0, 36), A.subtract)
+                    ts(f("s18", 0, 9), f("f18", 0, 9), -2.0, A.mult, 1.0, A.add)
                 table(t("oP%d" % (i + 1), 0, 5), f("Gs"), 80)
                 if i == 0:
-                    ts(f("fs", 0, 36), f("dj", 0, 36), pcol(9), A.mult, PAR4, A.add)
+                    tt(f("fM8", 0, 72), f("fl", 0, 72), f("M8", 0, 72), A.mult)
+                elif i == 1:
+                    tt(f("f18", 8, 9), f("f18", 8, 9), pcol(12), A.max)
+                else:
+                    scan(f("fS8", 0, 72), f("m8z", 0, 72), f("fM8", 0, 72), A.mult, A.add)
             else:
+                tt(f("x8", 15, 144, 16), f("tb", 0, 9), f("f18", 0, 9), A.add)
                 gop(lb, la, o, f("lc"), A.min)
             low = lb
-        gop(f("b"), low, t("oR", 0, 5), f("J"), A.not_equal)
+        ts(f("fs18", 0, 9), f("fS8", 7, 72, 8), pcol(10), A.mult, PAR2, A.add)
+        gop(f("b"), low, t("oR", 0, 5), f("J1"), A.not_equal)
         tt(f("a", 0, 72), (low[0], low[1], low[1] + 72, 1), f("JM2", 0, 72), A.is_equal)
-        tt(f("cd", 0, 72), f("a", 0, 72), f("b", 0, 72), A.mult)
-        tt(f("dc", 0, 36), f("cd", 0, 72, 2), f("cd", 1, 72, 2), A.add)
-        tt(f("dy", 0, 36), f("dc", 0, 36), f("dh", 0, 36), A.mult)
-        tt(f("tab", 0, 36), f("c1", 0, 36), f("dy", 0, 36), A.add)
-        tt(f("tab", 36, 72), f("c2", 0, 36), f("dy", 0, 36), A.subtract)
-        cp(t("tt4", 0, 36), f("tab", 0, 36))
-        cp(t("tt4", 36, 72), f("tab", 36, 72))
-        for h in range(2):
-            gop(t(Z, 576 * h, 576 * h + 576), t(XK), t("tt4", 36 * h, 36 * h + 36), t(XC, 576 * h, 576 * h + 576), A.add)
-            quant(t(zq, 144 * h, 144 * h + 144), t(zs, 144 * h, 144 * h + 144), t(Z, 576 * h, 576 * h + 576))
-            for b in range(4):
-                mm(bank(4 + 4 * h + b, 144), t("wq", 128 * b, 128 * b + 128), t("wp", 128 * b, 128 * b + 128),
-                   t(zq, 144 * h, 144 * h + 144), t(zs, 144 * h, 144 * h + 144))
-                if h == 0:
-                    act(t(H, b, 576, 4), bank(4 + b, 144), 0.03125)
-        quant(t(hq, 0, 144), t(hs, 0, 144), t(H, 0, 576))
+        tt(f("x4", 0, 144, 2), f("a", 0, 72), f("b", 0, 72), A.mult)
+        tt(f("z8", 15, 144, 16), f("fs18", 0, 9), f("s18", 0, 9), A.mult)
+        scan(f("xs4"), f("z4"), f("x4"), A.mult, A.add)
+        cp(t("tt4", 0, 36), f("xs4", 3, 144, 4))
+        tt(f("tab2", 0, 36), f("cc4", 0, 36), f("xs4", 3, 144, 4), A.subtract)
+        if r > 0:
+            actg(t(kk), t("kf%d" % r), t(kt), 1.0, -144.0)
+
+        def layer(i, a, b, at):
+            gop(t(Z, 4 * a, 4 * b), t(XK), t("tt4", a // 4, b // 4), t(XC, 4 * a, 4 * b), A.add)
+            if i == 0:
+                cp(t("tt4", 36, 72), f("tab2", 0, 36))
+            q, s = t(zq, 128 * i, 128 * i + 128), t(zs, 128 * i, 128 * i + 128)
+            quant(q, s, t(Z, 4 * (b - 128), 4 * b))
+            for k in range(4):
+                mm(bank(at + k, 128), t("wq", 128 * k, 128 * k + 128), t("wp", 128 * k, 128 * k + 128), q, s)
+                o, c = bank(at + k, 128), t(B if i == 2 else H, 4 * a + k, 4 * b, 4)
+                act(c, (o[0], o[2] - (b - a), o[2], 1), 0.03125)
+
+        layer(0, 0, C1, 4)
+        layer(1, C1, E, 8)
+        quant(t(hq, 0, C1), t(hs, 0, C1), t(H, 0, 4 * C1))
         dst = partner[r]
         n = send(dst, "ha%d" % r, t(lq, 0, C1), t(hq, 0, C1), [t(hq, 0, C1)], True)
         n += send(dst, "ha%d" % r, t(ls, 0, C1), t(hs, 0, C1), [t(hs, 0, C1)])
-        def second(b):
-            k = bank(8 + b, 144)
-            return (k[0], k[1], k[1] + C2, 1), (k[0], k[1] + C2, k[1] + 144, 1)
-        for b in range(4):
-            act(t(H, 576 + b, 896, 4), second(b)[0], 0.03125)
         if r == 0:
-            ts(f("m8z"), f("t8"), 0.0, A.is_gt)
-        tt(f("fM8", 0, 72), f("fl", 0, 72), f("M8", 0, 72), A.mult)
+            constants3()
         tt(f("a8", 0, 72), (low[0], low[1], low[1] + 72, 1), f("JM8", 0, 72), A.is_equal)
-        tt(f("f18", 0, 9), sd, f("sgT", 0, 9), A.mult)
-        scan(f("fS8", 0, 72), f("m8z", 0, 72), f("fM8", 0, 72), A.mult, A.add)
-        tt(f("f18", 8, 9), f("f18", 8, 9), pcol(12), A.max)
-        ts(f("fs18", 0, 9), f("fS8", 7, 72, 8), pcol(10), A.mult, PAR2, A.add)
+        tt(f("x8", 0, 144, 2), f("a8", 0, 72), f("b", 0, 72), A.mult)
         quant(t(hq, C1, C1 + 128), t(hs, C1, C1 + 128), t(H, 4 * (E - 128), 4 * E))
         m = send(dst, "hb%d" % r, t(lq, C1, E), t(hq, C1 + 128 - C2, C1 + 128), [t(hq, C1, C1 + 128)], True)
         m += send(dst, "hb%d" % r, t(ls, C1, E), t(hs, C1 + 128 - C2, C1 + 128), [t(hs, C1, C1 + 128)])
         arrives("ha%d" % r, n, [t(lq, 0, C1), t(ls, 0, C1)])
         arrives("hb%d" % r, m, [t(lq, C1, E), t(ls, C1, E)])
-        for b in range(4):
-            act(t(B, 4 * E + b, 4 * C, 4), second(b)[1], 0.03125)
+        scan(f("xs8"), f("z8"), f("x8"), A.mult, A.add)
+        layer(2, E, C, 12)
         if r == 0:
-            constants3()
-        kf, lk = "kf%d" % r, "lk%d" % r
-        for i in range(16):
-            dma("y", "df%d" % r, T[kf][i:128:16, :], T[lk][:, :], [t(lk)], [(kf, i, C, 16)])
-        tt(f("c8", 0, 72), f("a8", 0, 72), f("b", 0, 72), A.mult)
-        ts(f("s18", 0, 9), f("f18", 0, 9), -2.0, A.mult, 1.0, A.add)
-        scan(f("cS8", 0, 72), f("m8z", 0, 72), f("c8", 0, 72), A.mult, A.add)
-        tt(f("h18", 0, 9), f("fs18", 0, 9), f("s18", 0, 9), A.mult)
-        tt(f("dy18", 0, 9), f("h18", 0, 9), f("cS8", 7, 72, 8), A.mult)
-        tt(f("f18", 0, 9), f("f18", 0, 9), f("dy18", 0, 9), A.add)
-        tt(f("tab18", 0, 9), f("tb", 0, 9), f("f18", 0, 9), A.add)
-        tt(f("tab18", 9, 18), f("tb", 9, 18), f("f18", 0, 9), A.subtract)
-        cp(t("tt18"), f("tab18", 0, 18))
+            constants4()
+        tt(f("up", 0, 9), f("cc18", 0, 9), f("xs8", 15, 144, 16), A.subtract)
+        cp(t("tt18", 0, 9), f("xs8", 15, 144, 16))
+        cp(t("tt18", 9, 18), f("up", 0, 9))
         if r == 0:
-            gat(t(kk), t(kf), t("ks"))
-        else:
-            actg(t(kk), t(kf), t(kt))
+            ts(t("ki", 0, 18), t("kli"), 15, A.bitwise_and)
+            ts(t("ki", 18, 36), t("kli"), 4, A.arith_shift_right)
+            ts(t("ki", 0, 18), t("ki", 0, 18), 18, A.mult)
+            tt(t("ki", 36, 54), t("ki", 0, 18), t("ki", 18, 36), A.add)
+            cp(t("ks"), t("ki", 36, 54))
+            gop(t(kk), t(kf), t("ks"), f("m144"), A.add)
         gop(f("n4w"), t(kk), t("tt18"), f("M4n"), A.add)
-        actg(t(nf), t(kk), t("tt18"))
+        actg(t(nf), t(kk), t("tt18"), 1.0, 144.0)
         scan(f("n4s"), f("d4"), f("n4w"), A.min, A.max)
         if r < 2:
             gop(f("n16w"), t(kk), t("tt18"), f("M16n"), A.add)
-        ts(t(nt), f("n4s", 3, 288, 4), 4.0, A.mult, P4, A.add)
+        ts(t(nt), f("n4s", 3, 288, 4), 4.0, A.mult, pcol(15), A.add)
         if r < 2:
-            scan(f("n16s"), f("d16"), f("n16w"), A.min, A.max)
-            table(t("kt%d" % (r + 1)), f("n16s"), 288)
+            scan(f("n16s"), f("d16b"), f("n16w"), A.min, A.max)
+            ts(t("kt%d" % (r + 1)), f("n16s", 15, 288, 16), 144.0, A.add)
             nd = "nd%d" % (r + 1)
             dma("y", "dn%d" % (r + 1), T[nd][:, :], T[nf][0:128:16, :], [t(nf)], [t(nd)])
             lr = "lr%d" % (r + 1)
@@ -504,7 +526,7 @@ def rank_program(g, core, T, topo):
         if r == 0:
             quant(t("eq"), t("es"), t("et"))
             quant(t("vq"), t("vs"), t("vb"))
-        for c0, c1, new, at in ((0, C1, 0, 12), (E - 128, E, 128 - C2, 16)):
+        for c0, c1, new, at in ((0, C1, 0, 16), (E - 128, E, 128 - C2, 20)):
             for b in range(4):
                 mm(bank(at + b, c1 - c0), t("eq", 128 * b, 128 * b + 128), t("es", 128 * b, 128 * b + 128), t(lq, c0, c1), t(ls, c0, c1))
                 k = bank(at + b, c1 - c0)
@@ -514,6 +536,7 @@ def rank_program(g, core, T, topo):
         Xn = "X%d" % (r + 1)
         for h in range(2):
             gop(t(Xn, 576 * h, 576 * h + 576), t(B), t(nt, 36 * h, 36 * h + 36), t(X, 576 * h, 576 * h + 576), A.add)
+        for h in range(2):
             state(r + 1, h)
             if r == 2:
                 q, s = "xq3", "xs3"

@@ -3,6 +3,7 @@ from concourse.mybir import dt, AluOpType, AxisListType, ActivationFunctionType
 
 C, HALF, E = 288, 144, 224
 MASKS = [4, 1, 2]
+HS = ((0, 160), (160, 288))
 C1 = 128
 C2 = E - C1
 F4 = "float8_e4m3fn_x4"
@@ -22,7 +23,7 @@ SCRATCH = {
     "kf0": ("sbuf", [128, C], "int32"), "kf1": ("sbuf", [128, C], "float32"), "kf2": ("sbuf", [128, C], "float32"),
     "pI": ("sbuf", [128, 8], "int32"), "uI": ("sbuf", [128, 8], "int32"), "pF": ("sbuf", [128, 24], "float32"),
     "uo": ("sbuf", [128, 8], "uint16"),
-    "ks": ("sbuf", [128, 18], "uint16"), "k4t": ("sbuf", [128, 80], "uint16"),
+    "ks": ("sbuf", [128, 18], "uint16"),
     "oAD": ("sbuf", [128, 10], "uint16"), "oBC": ("sbuf", [128, 10], "uint16"), "oRi": ("sbuf", [128, 6], "uint16"),
     "o4": ("sbuf", [128, 4], "uint16"), "oVC": ("sbuf", [128, 6], "uint16"), "oR": ("sbuf", [128, 6], "uint16"),
     "tt4": ("sbuf", [128, 72], "uint16"), "tt18": ("sbuf", [128, 18], "uint16"),
@@ -41,13 +42,13 @@ for _i in range(3):
     SCRATCH["Z%d" % _i] = ("sbuf", [128, 4 * C], "bfloat16")
     SCRATCH["H%d" % _i] = ("sbuf", [128, 4 * E], "bfloat16")
     SCRATCH["B%d" % _i] = ("sbuf", [128, 4 * C], "bfloat16")
-    SCRATCH["zq%d" % _i] = ("sbuf", [128, 384], F4)
-    SCRATCH["zs%d" % _i] = ("sbuf", [128, 384], "uint8")
+    SCRATCH["zq%d" % _i] = ("sbuf", [128, C1 + 256], F4)
+    SCRATCH["zs%d" % _i] = ("sbuf", [128, C1 + 256], "uint8")
     SCRATCH["hq%d" % _i] = ("sbuf", [128, C1 + 128], F4)
     SCRATCH["hs%d" % _i] = ("sbuf", [128, C1 + 128], "uint8")
     SCRATCH["lq%d" % _i] = ("sbuf", [128, E], F4)
     SCRATCH["ls%d" % _i] = ("sbuf", [128, E], "uint8")
-    SCRATCH["nt%d" % _i] = ("sbuf", [128, 72], "uint16")
+    SCRATCH["k4t%d" % _i] = ("sbuf", [128, 80], "uint16")
     SCRATCH["nf%d" % _i] = ("sbuf", [128, C], "float32")
     SCRATCH["kk%d" % _i] = ("sbuf", [128, C], "float32")
 _ROWS = {
@@ -58,8 +59,8 @@ _ROWS = {
     "b1": 40, "cc4": 40, "bits": 288, "fl": 144, "BC": 16, "tw": 32, "ts": 32,
     "Vw": 80, "Vs": 80, "Vb": 80, "F0": 80, "F1": 80, "F2": 80, "G0": 80, "G1": 80, "G2": 80,
     "l0": 80, "l1": 80, "l2": 80, "l3": 80, "l4": 80, "l5": 80, "l6": 80, "l7": 80, "lc": 80,
-    "fM2": 80, "dj": 40, "s1": 40, "fs": 40, "a": 80, "b": 80, "x4": 144, "z4": 144, "xs4": 144, "tab2": 40,
-    "fM8": 80, "fS8": 80, "a8": 80, "f18": 16, "s18": 16, "fs18": 16, "x8": 144, "z8": 144, "xs8": 144, "up": 16,
+    "fM2": 80, "dj": 40, "s1": 40, "fs": 40, "x4": 240, "z4": 216, "xs4": 216, "tab2": 40,
+    "fM8": 80, "fS8": 80, "f18": 16, "s18": 16, "fs18": 16, "x8": 240, "z8": 216, "xs8": 216, "up": 16,
 }
 _ROWS2 = {
     "x2": 288, "z2": 288, "xs2": 288, "n4w": 288, "n4s": 288, "n16w": 288, "n16s": 288, "d4": 288, "d16b": 288,
@@ -222,10 +223,10 @@ def rank_program(g, core, T, topo):
         total[sem] = total.get(sem, 0) + n
         note(sem, 0, [], writes)
 
-    dma("y", "dx0", T.X0[:, 0:576], T.x[:, 0:576], [], [t("X0", 0, 576)])
+    dma("y", "dx0", T.X0[:, 0:640], T.x[:, 0:640], [], [t("X0", 0, 640)])
     dma("s", "dk", T.kli[:, :], T.kl[:, :], [], [t("kli")])
     dma("s", "du", T.ub[:, :], T.u[:, :], [], [t("ub")])
-    dma("y", "dx1", T.X0[:, 576:1152], T.x[:, 576:1152], [], [t("X0", 576, 1152)])
+    dma("y", "dx1", T.X0[:, 640:1152], T.x[:, 640:1152], [], [t("X0", 640, 1152)])
     dma("y", "dkl", T.kld[:, :], T.kl[:, :], [], [t("kld")])
     need("y", "dx1", 16)
     dma("y", "dw", T.wq[:, 0:512].bitcast(dt.uint8), T.wc[:, :], [], [t("wq")])
@@ -264,7 +265,8 @@ def rank_program(g, core, T, topo):
     equal(f("M16n"), f("t16"), P16, f("tmp"))
     act(f("sgM", 0, 72), f("M16n", 0, 72))
     act(f("sgM", 72, 144), f("M16n", 72, 144), -1.0)
-    actf(f("m144"), f("t16"), IDENT, 0.0, -144.0)
+    actf(f("z2"), f("t32"), SIGN, 1.0, 0.0)
+    actf(f("d16"), f("t16", 0, 80), SIGN, 1.0, 0.0)
     fill(f("x2"), 0.0)
     ts(f("cT", 0, 9), f("q16", 0, 9), P16, A.add)
     ts(f("tA", 0, 9), f("cT", 0, 9), 36.0, A.is_ge, 72.0, A.mult)
@@ -278,20 +280,22 @@ def rank_program(g, core, T, topo):
     tt(f("tcAD", 0, 9), f("tA", 0, 9), f("tD", 0, 9), A.add)
     tt(f("tcBC", 0, 9), f("tcAD", 0, 9), f("sgT", 0, 9), A.add)
     ts(f("x2", 31, 288, 32), f("tcAD", 0, 9), -144.0, A.add)
-    run("v", lambda: g.vector.memset(T.one[:, 0:512], 1.0), [], [t("one")])
-    for e in range(4):
-        run("q", lambda: g.affine_select(T.et[:, 512 * e:512 * e + 512], T.one[:, 0:512], [[-1, 512]], A.is_equal, 0.0, e, 4),
-            [t("one")], [t("et", 512 * e, 512 * e + 512)])
-    cp(t("kt0"), t("kli"))
-    for e in range(4):
-        ts(t("k4t", 20 * e, 20 * e + 18), t("kli"), 4, A.mult, e, A.add)
-    actf(f("z2"), f("t32"), SIGN, 1.0, 0.0)
-    equal(f("M2"), f("t2"), I8, f("tmp", 0, 80))
-    equal(f("M8"), f("t8"), I2, f("tmp", 80, 160))
-    act(f("J2"), f("J1"))
+
+    def state(r, h):
+        a, b = HS[h]
+        quant(t("xq%d" % r, a, b), t("xs%d" % r, a, b), t("X%d" % r, 4 * a, 4 * b))
+
+    def scores(r, h):
+        a, b = HS[h]
+        mm(bank(2 + h, b - a), t("ur"), t("urs"), t("xq%d" % r, a, b), t("xs%d" % r, a, b))
+
     fill(f("x4"), 0.0)
+    fill(f("z4"), -1.0)
     fill(f("x8"), 0.0)
+    fill(f("z8"), -1.0)
     quant(t("uq"), t("us"), t("ub"))
+    state(0, 0)
+    state(0, 1)
     run("v", lambda: g.vector.tensor_copy(T.ur[:, 0:128].bitcast(dt.uint32), T.uq[:, 0:128].bitcast(dt.uint32).indirect(T.uo[:, 0:8])),
         [t("uq"), t("uo")], [t("ur")])
     run("s", lambda: g.scalar.activation(T.urs[:, 0:128], T.us[:, 0:128].indirect(T.uo[:, 0:8]), COPY), [t("us"), t("uo")], [t("urs")])
@@ -300,22 +304,22 @@ def rank_program(g, core, T, topo):
         act(f(n, 0, 72), f("W1", 0, 72))
         act(f(n, 216, 288), f("W1", 216, 288))
 
+    actf(f("d16"), f("d16"), IDENT, 16384.0, -8192.0)
+    actf(f("M16n"), f("M16n"), IDENT, 4096.0, -4096.0)
     ends("W2")
+    act(f("d16b", 0, 80), f("d16"))
     ends("W3")
+    act(f("J2"), f("J1"))
 
-    def state(r, h):
-        quant(t("xq%d" % r, 144 * h, 144 * h + 144), t("xs%d" % r, 144 * h, 144 * h + 144), t("X%d" % r, 576 * h, 576 * h + 576))
-        if r < 3:
-            mm(bank(2 + h, 144), t("ur"), t("urs"), t("xq%d" % r, 144 * h, 144 * h + 144), t("xs%d" % r, 144 * h, 144 * h + 144))
-
-    state(0, 0)
-    state(0, 1)
-
-    def constants1():
-        ts(f("M16n"), f("M16n"), -1.0, A.add, 4096.0, A.mult)
-        ts(f("d16"), f("t16", 0, 80), 0.0, A.is_gt, 16384.0, A.mult)
-        ts(f("d16"), f("d16"), -8192.0, A.add)
-        cp(f("d16b", 0, 80), f("d16"))
+    scores(0, 0)
+    scores(0, 1)
+    cp(t("kt0"), t("kli"))
+    for e in range(4):
+        ts(t("k4t0", 20 * e, 20 * e + 18), t("kli"), 4, A.mult, e, A.add)
+    run("v", lambda: g.vector.memset(T.one[:, 0:512], 1.0), [], [t("one")])
+    for e in range(4):
+        run("q", lambda: g.affine_select(T.et[:, 512 * e:512 * e + 512], T.one[:, 0:512], [[-1, 512]], A.is_equal, 0.0, e, 4),
+            [t("one")], [t("et", 512 * e, 512 * e + 512)])
 
     def constants2():
         ts(t("pF", 16, 20), f("t4", 0, 4), I4, A.is_equal, 4.0, A.mult)
@@ -331,15 +335,10 @@ def rank_program(g, core, T, topo):
 
     def constants3():
         ts(pcol(14), P16, 0.0, A.is_equal)
-        ts(pcol(15), P4, 576.0, A.add)
         tt(f("JM8"), f("J1"), f("M8"), A.mult)
         tt(f("JM8", 0, 1), f("JM8", 0, 1), pcol(14), A.subtract)
 
     def constants4():
-        ts(f("M4n"), f("t4"), I4, A.is_equal)
-        ts(f("tmp"), f("t4"), 0.0, A.is_gt, 16384.0, A.mult)
-        ts(f("M4n"), f("M4n"), -1.0, A.add, 4096.0, A.mult)
-        ts(f("d4"), f("tmp"), -8192.0, A.add)
         ts(f("tmp"), f("t16"), 0.0, A.is_gt, 16384.0, A.mult)
         ts(f("d16b"), f("tmp"), -8192.0, A.add)
 
@@ -348,29 +347,25 @@ def rank_program(g, core, T, topo):
 
     for r in range(3):
         X, XK, XC, Z, H, B, kt = ["%s%d" % (n, r) for n in ("X", "XK", "XC", "Z", "H", "B", "kt")]
-        zq, zs, hq, hs, lq, ls, nt, nf, kk = ["%s%d" % (n, r) for n in ("zq", "zs", "hq", "hs", "lq", "ls", "nt", "nf", "kk")]
+        zq, zs, hq, hs, lq, ls, nf, kk = ["%s%d" % (n, r) for n in ("zq", "zs", "hq", "hs", "lq", "ls", "nf", "kk")]
         kf, lk = "kf%d" % r, "lk%d" % r
         for i in range(16):
             dma("y", "df%d" % r, T[kf][i:128:16, :], T[lk][:, :], [t(lk)], [(kf, i, C, 16)])
-        if r == 0:
-            constants1()
         for h in range(2):
-            ts(f("bits", 144 * h, 144 * h + 144), bank(2 + h, 144), 0.0, A.is_gt)
+            ts(f("bits", HS[h][0], HS[h][1]), bank(2 + h, HS[h][1] - HS[h][0]), 0.0, A.is_gt)
         actg(f("fl"), f("bits"), t(kt, 0, 9))
 
         def half_of_xk(h):
-            if r == 0:
-                for e in (2 * h, 2 * h + 1):
-                    actg(t(XK, e, 1152, 4), t(X), t("k4t", 20 * e, 20 * e + 18), 0.5)
-            else:
-                actg(t(XK, 576 * h, 576 * h + 576), t(X), t("nt%d" % (r - 1), 36 * h, 36 * h + 36), 0.5)
+            for e in (2 * h, 2 * h + 1):
+                actg(t(XK, e, 1152, 4), t(X), t("k4t%d" % r, 20 * e, 20 * e + 18), 0.5)
 
         half_of_xk(0)
         if r == 0:
             ends("W4")
             ends("W5")
+            for m, c, i, o in (("M2", "t2", I8, 0), ("M8", "t8", I2, 80)):
+                equal(f(m), f(c), i, f("tmp", o, o + 80))
             actf(f("m4z"), f("t4", 0, 144), SIGN, 1.0, 0.0)
-            actf(f("z4"), f("t4", 0, 144), SIGN, 1.0, 0.0)
         gop(f("x2", 0, 288, 2), f("bits"), t(kt, 0, 9), f("sgM"), A.mult)
         scan(f("xs2"), f("z2"), f("x2"), A.mult, A.add)
         sd = f("xs2", 30, 288, 32)
@@ -386,24 +381,37 @@ def rank_program(g, core, T, topo):
             constants2()
         gop(f("tw", 0, 16), f("W3"), t("oAD", 0, 1), f("M16n", 0, 16), A.add)
         gop(f("tw", 16, 32), f("W3"), t("oAD", 8, 9), f("M16n", 0, 16), A.add)
-        for i in range(4):
-            acts(f("fM4", i, 144, 4), f("fl", i, 144, 4), pcol(16 + i))
-        act(f("fM4", 143, 144), pcol(19))
-        for i in range(2):
-            acts(f("fM2", i, 72, 2), f("fl", i, 72, 2), pcol(20 + i))
+        def masks():
+            for i in range(4):
+                acts(f("fM4", i, 144, 4), f("fl", i, 144, 4), pcol(16 + i))
+            act(f("fM4", 143, 144), pcol(19))
+            for i in range(2):
+                acts(f("fM2", i, 72, 2), f("fl", i, 72, 2), pcol(20 + i))
+        if r > 0:
+            masks()
         actg(f("W4", 72, 216), f("W3"), t("oAD", 0, 9))
         actg(f("W5", 72, 216), f("W3"), t("oAD", 0, 9))
         if r == 0:
-            actf(f("z8"), f("t16", 0, 144), SIGN, 1.0, 0.0)
+            masks()
+        def late():
+            actf(f("m144"), f("t16"), IDENT, 0.0, -144.0)
+            actf(f("z4", 0, 216, 6), f("q32", 0, 36), IDENT, 0.0, 0.0)
+            actf(f("z4", 2, 216, 6), f("q32", 0, 36), IDENT, 0.0, 1.0)
+            actf(f("z8", 2, 216, 3), f("t2", 0, 72), IDENT, 0.0, 1.0)
+            actf(f("z8", 0, 216, 24), f("q16", 0, 9), IDENT, 0.0, 0.0)
             actf(f("m8z"), f("t8"), SIGN, 1.0, 0.0)
             actf(f("tb", 0, 9), f("cT", 0, 9), IDENT, 2.0, 0.0)
             actf(f("cc18", 0, 9), f("cT", 0, 9), IDENT, 4.0, 1.0)
-        half_of_xk(1)
+        if r > 0:
+            half_of_xk(1)
         scan(f("ts"), f("d16", 0, 32), f("tw"), A.min, A.max)
         cp(t("o4", 0, 4, 2), f("ts", 15, 32, 16))
-        scan(f("fS4"), f("m4z"), f("fM4"), A.mult, A.add)
+        if r > 0:
+            scan(f("fS4"), f("m4z"), f("fM4"), A.mult, A.add)
         gat(f("W5", 72, 88), f("W4"), t("o4", 0, 1))
         gat(f("W5", 200, 216), f("W4"), t("o4", 2, 3))
+        if r == 0:
+            scan(f("fS4"), f("m4z"), f("fM4"), A.mult, A.add)
         tt(f("dj", 0, 36), f("fM2", 0, 72, 2), f("fM2", 1, 72, 2), A.add)
         gop(f("Vw"), f("W5"), t("oBC", 0, 5), f("M16n", 0, 80), A.add)
         actg(f("Vb"), f("W5"), t("oBC", 4, 9))
@@ -415,7 +423,9 @@ def rank_program(g, core, T, topo):
         ts(f("fs", 0, 36), f("dj", 0, 36), pcol(9), A.mult, PAR4, A.add)
         gop(f("Pw"), f("Vb"), t("oVC", 0, 5), f("M16n", 0, 80), A.add)
         actg(f("F0"), f("Vb"), t("oVC", 0, 5))
-        tt(f("x4", 3, 144, 4), f("b1", 0, 36), f("fS4", 3, 144, 4), A.add)
+        if r == 0:
+            late()
+        tt(f("x4", 5, 216, 6), f("b1", 0, 36), f("fS4", 3, 144, 4), A.add)
         scan(f("Ps"), f("d16b", 0, 80), f("Pw"), A.min, A.max)
         ts(t("oR", 0, 5), f("Rs", 15, 80, 16), 71.0, A.min)
         table(t("oP0", 0, 5), f("Ps"), 80)
@@ -435,13 +445,15 @@ def rank_program(g, core, T, topo):
                 if i < 2:
                     actg(f("F%d" % (i + 1)), Gi, o)
                 act(f("lc"), lb)
-                if i == 1:
+                if r == 0 and i < 2:
+                    actg(t(XK, 2 + i, 1152, 4), t(X), t("k4t0", 40 + 20 * i, 58 + 20 * i), 0.5)
+                if i == (1 if r else 2):
                     act(t(XC, 0, 576), t(XK, 0, 576))
                 if i == 2:
                     act(t(XC, 576, 1152), t(XK, 576, 1152))
                 scan(f("Gs"), f("d16b", 0, 80), f("Gw"), A.min, A.max)
                 if i == 0:
-                    tt(f("z4", 3, 144, 4), f("s1", 0, 36), f("fs", 0, 36), A.mult)
+                    tt(f("z4", 5, 216, 6), f("s1", 0, 36), f("fs", 0, 36), A.mult)
                 elif i == 1:
                     tt(f("f18", 0, 9), sd, f("sgT", 0, 9), A.mult)
                 else:
@@ -454,17 +466,16 @@ def rank_program(g, core, T, topo):
                 else:
                     scan(f("fS8", 0, 72), f("m8z", 0, 72), f("fM8", 0, 72), A.mult, A.add)
             else:
-                tt(f("x8", 15, 144, 16), f("tb", 0, 9), f("f18", 0, 9), A.add)
+                tt(f("x8", 23, 216, 24), f("tb", 0, 9), f("f18", 0, 9), A.add)
                 gop(lb, la, o, f("lc"), A.min)
             low = lb
         ts(f("fs18", 0, 9), f("fS8", 7, 72, 8), pcol(10), A.mult, PAR2, A.add)
-        gop(f("b"), low, t("oR", 0, 5), f("J1"), A.not_equal)
-        tt(f("a", 0, 72), (low[0], low[1], low[1] + 72, 1), f("JM2", 0, 72), A.is_equal)
-        tt(f("x4", 0, 144, 2), f("a", 0, 72), f("b", 0, 72), A.mult)
-        tt(f("z8", 15, 144, 16), f("fs18", 0, 9), f("s18", 0, 9), A.mult)
-        scan(f("xs4"), f("z4"), f("x4"), A.mult, A.add)
-        cp(t("tt4", 0, 36), f("xs4", 3, 144, 4))
-        tt(f("tab2", 0, 36), f("cc4", 0, 36), f("xs4", 3, 144, 4), A.subtract)
+        gop(f("x4", 0, 240, 3), low, t("oR", 0, 5), f("JM2"), A.is_equal)
+        tt(f("x4", 1, 216, 3), (low[0], low[1], low[1] + 72, 1), f("JM2", 0, 72), A.is_equal)
+        tt(f("z8", 23, 216, 24), f("fs18", 0, 9), f("s18", 0, 9), A.mult)
+        scan(f("xs4"), f("z4"), f("x4", 0, 216), A.mult, A.add)
+        cp(t("tt4", 0, 36), f("xs4", 5, 216, 6))
+        tt(f("tab2", 0, 36), f("cc4", 0, 36), f("xs4", 5, 216, 6), A.subtract)
         if r > 0:
             actg(t(kk), t("kf%d" % r), t(kt), 1.0, -144.0)
 
@@ -472,11 +483,13 @@ def rank_program(g, core, T, topo):
             gop(t(Z, 4 * a, 4 * b), t(XK), t("tt4", a // 4, b // 4), t(XC, 4 * a, 4 * b), A.add)
             if i == 0:
                 cp(t("tt4", 36, 72), f("tab2", 0, 36))
-            q, s = t(zq, 128 * i, 128 * i + 128), t(zs, 128 * i, 128 * i + 128)
-            quant(q, s, t(Z, 4 * (b - 128), 4 * b))
+            n = max(128, b - a)
+            p = 0 if i == 0 else C1 + 128 * (i - 1)
+            q, s = t(zq, p, p + n), t(zs, p, p + n)
+            quant(q, s, t(Z, 4 * (b - n), 4 * b))
             for k in range(4):
-                mm(bank(at + k, 128), t("wq", 128 * k, 128 * k + 128), t("wp", 128 * k, 128 * k + 128), q, s)
-                o, c = bank(at + k, 128), t(B if i == 2 else H, 4 * a + k, 4 * b, 4)
+                mm(bank(at + k, n), t("wq", 128 * k, 128 * k + 128), t("wp", 128 * k, 128 * k + 128), q, s)
+                o, c = bank(at + k, n), t(B, C * k + a, C * k + b) if i == 2 else t(H, 4 * a + k, 4 * b, 4)
                 act(c, (o[0], o[2] - (b - a), o[2], 1), 0.03125)
 
         layer(0, 0, C1, 4)
@@ -487,19 +500,19 @@ def rank_program(g, core, T, topo):
         n += send(dst, "ha%d" % r, t(ls, 0, C1), t(hs, 0, C1), [t(hs, 0, C1)])
         if r == 0:
             constants3()
-        tt(f("a8", 0, 72), (low[0], low[1], low[1] + 72, 1), f("JM8", 0, 72), A.is_equal)
-        tt(f("x8", 0, 144, 2), f("a8", 0, 72), f("b", 0, 72), A.mult)
+        tt(f("x8", 1, 216, 3), (low[0], low[1], low[1] + 72, 1), f("JM8", 0, 72), A.is_equal)
+        gop(f("x8", 0, 240, 3), low, t("oR", 0, 5), f("JM8"), A.is_equal)
         quant(t(hq, C1, C1 + 128), t(hs, C1, C1 + 128), t(H, 4 * (E - 128), 4 * E))
         m = send(dst, "hb%d" % r, t(lq, C1, E), t(hq, C1 + 128 - C2, C1 + 128), [t(hq, C1, C1 + 128)], True)
         m += send(dst, "hb%d" % r, t(ls, C1, E), t(hs, C1 + 128 - C2, C1 + 128), [t(hs, C1, C1 + 128)])
         arrives("ha%d" % r, n, [t(lq, 0, C1), t(ls, 0, C1)])
         arrives("hb%d" % r, m, [t(lq, C1, E), t(ls, C1, E)])
-        scan(f("xs8"), f("z8"), f("x8"), A.mult, A.add)
+        scan(f("xs8"), f("z8"), f("x8", 0, 216), A.mult, A.add)
         layer(2, E, C, 12)
         if r == 0:
             constants4()
-        tt(f("up", 0, 9), f("cc18", 0, 9), f("xs8", 15, 144, 16), A.subtract)
-        cp(t("tt18", 0, 9), f("xs8", 15, 144, 16))
+        tt(f("up", 0, 9), f("cc18", 0, 9), f("xs8", 23, 216, 24), A.subtract)
+        cp(t("tt18", 0, 9), f("xs8", 23, 216, 24))
         cp(t("tt18", 9, 18), f("up", 0, 9))
         if r == 0:
             ts(t("ki", 0, 18), t("kli"), 15, A.bitwise_and)
@@ -508,15 +521,13 @@ def rank_program(g, core, T, topo):
             tt(t("ki", 36, 54), t("ki", 0, 18), t("ki", 18, 36), A.add)
             cp(t("ks"), t("ki", 36, 54))
             gop(t(kk), t(kf), t("ks"), f("m144"), A.add)
-        gop(f("n4w"), t(kk), t("tt18"), f("M4n"), A.add)
+        gop(f("n16w"), t(kk), t("tt18"), f("M16n"), A.add)
         actg(t(nf), t(kk), t("tt18"), 1.0, 144.0)
-        scan(f("n4s"), f("d4"), f("n4w"), A.min, A.max)
+        scan(f("n16s"), f("d16b"), f("n16w"), A.min, A.max)
+        ts(t("kt%d" % (r + 1)), f("n16s", 15, 288, 16), 144.0, A.add)
         if r < 2:
-            gop(f("n16w"), t(kk), t("tt18"), f("M16n"), A.add)
-        ts(t(nt), f("n4s", 3, 288, 4), 4.0, A.mult, pcol(15), A.add)
-        if r < 2:
-            scan(f("n16s"), f("d16b"), f("n16w"), A.min, A.max)
-            ts(t("kt%d" % (r + 1)), f("n16s", 15, 288, 16), 144.0, A.add)
+            for e in range(4):
+                ts(t("k4t%d" % (r + 1), 20 * e, 20 * e + 18), f("n16s", 15, 288, 16), 4.0, A.mult, 576.0 + e, A.add)
             nd = "nd%d" % (r + 1)
             dma("y", "dn%d" % (r + 1), T[nd][:, :], T[nf][0:128:16, :], [t(nf)], [t(nd)])
             lr = "lr%d" % (r + 1)
@@ -531,21 +542,22 @@ def rank_program(g, core, T, topo):
                 mm(bank(at + b, c1 - c0), t("eq", 128 * b, 128 * b + 128), t("es", 128 * b, 128 * b + 128), t(lq, c0, c1), t(ls, c0, c1))
                 k = bank(at + b, c1 - c0)
                 k = (k[0], k[1] + new, k[2], 1)
-                o = t(B, 4 * (c0 + new) + b, 4 * c1, 4)
-                act(o, k)
+                act(t(B, C * b + c0 + new, C * b + c1), k)
         Xn = "X%d" % (r + 1)
-        for h in range(2):
-            gop(t(Xn, 576 * h, 576 * h + 576), t(B), t(nt, 36 * h, 36 * h + 36), t(X, 576 * h, 576 * h + 576), A.add)
+        for e, a, b in ((0, 0, C), (1, 0, C), (2, 0, C), (3, 0, HS[0][1]), (3, HS[1][0], C)):
+            gop(t(Xn, 4 * a + e, 4 * b, 4), t(B, C * e, C * e + C), t("kt%d" % (r + 1), a // 16, b // 16), t(X, 4 * a + e, 4 * b, 4), A.add)
         for h in range(2):
             state(r + 1, h)
+            if r < 2:
+                scores(r + 1, h)
             if r == 2:
                 q, s = "xq3", "xs3"
-                a, b = 144 * h, 144 * h + 144
-                mm(bank(2 + h, 144), t("vq"), t("vs"), t(q, a, b), t(s, a, b))
+                a, b = HS[h]
+                mm(bank(2 + h, b - a), t("vq"), t("vs"), t(q, a, b), t(s, a, b))
                 dma("y", "dout", T.oc[:, 4 * a:4 * b], T[q][:, a:b].bitcast(dt.uint8), [t(q, a, b)], [])
                 for i in range(4):
                     dma("y", "dout", T.osc[4 * i:4 * i + 4, a:b], T[s][32 * i:32 * i + 4, a:b], [t(s, a, b)], [])
-                act(t("ysb", a, b), bank(2 + h, 144))
+                act(t("ysb", a, b), bank(2 + h, b - a))
                 dma("s", "dout", T.y[:, a:b], T.ysb[:, a:b], [t("ysb", a, b)], [])
     need("y", "dout", total["dout"])
     need("q", "sent", total["sent"])

from concourse.bass import DstId, RemoteDMATransfer
from concourse.mybir import dt, AluOpType, AxisListType, ActivationFunctionType

C, HALF, E = 288, 144, 224
MASKS = [4, 1, 2]
HS = ((0, 160), (160, 288))
C1 = 128
C2 = E - C1
F4 = "float8_e4m3fn_x4"

SCRATCH = {
    "ub": ("sbuf", [128, 512], "bfloat16"), "vb": ("sbuf", [128, 512], "bfloat16"), "et": ("sbuf", [128, 2048], "bfloat16"),
    "one": ("sbuf", [128, 512], "bfloat16"),
    "uq": ("sbuf", [128, 128], F4), "us": ("sbuf", [128, 128], "uint8"),
    "ur": ("sbuf", [128, 128], F4), "urs": ("sbuf", [128, 128], "uint8"),
    "vq": ("sbuf", [128, 128], F4), "vs": ("sbuf", [128, 128], "uint8"),
    "eq": ("sbuf", [128, 512], F4), "es": ("sbuf", [128, 512], "uint8"),
    "wq": ("sbuf", [128, 512], F4), "wp": ("sbuf", [128, 512], "uint8"),
    "kli": ("sbuf", [128, 18], "int32"), "ki": ("sbuf", [128, 54], "int32"),
    "kld": ("dram", [128, 18], "int32"), "lk0": ("dram", [128, 18], "int32"),
    "nd1": ("dram", [128, 18], "float32"), "nd2": ("dram", [128, 18], "float32"),
    "lk1": ("dram", [128, 18], "float32"), "lk2": ("dram", [128, 18], "float32"),
    "kf0": ("sbuf", [128, C], "int32"), "kf1": ("sbuf", [128, C], "float32"), "kf2": ("sbuf", [128, C], "float32"),
    "pI": ("sbuf", [128, 8], "int32"), "uI": ("sbuf", [128, 8], "int32"), "pF": ("sbuf", [128, 24], "float32"),
    "uo": ("sbuf", [128, 8], "uint16"),
    "ks": ("sbuf", [128, 18], "uint16"),
    "oAD": ("sbuf", [128, 10], "uint16"), "oBC": ("sbuf", [128, 10], "uint16"), "oRi": ("sbuf", [128, 6], "uint16"),
    "o4": ("sbuf", [128, 4], "uint16"), "oVC": ("sbuf", [128, 6], "uint16"), "oR": ("sbuf", [128, 6], "uint16"),
    "tt4": ("sbuf", [128, 72], "uint16"), "tt18": ("sbuf", [128, 18], "uint16"),
    "ps": ("psum", [128, 4096], "float32"),
    "ysb": ("sbuf", [128, C], "float32"),
}
for _i in range(4):
    SCRATCH["X%d" % _i] = ("sbuf", [128, 4 * C], "bfloat16")
    SCRATCH["xq%d" % _i] = ("sbuf", [128, C], F4)
    SCRATCH["xs%d" % _i] = ("sbuf", [128, C], "uint8")
    SCRATCH["oP%d" % _i] = ("sbuf", [128, 6], "uint16")
    SCRATCH["kt%d" % _i] = ("sbuf", [128, 18], "uint16")
for _i in range(3):
    SCRATCH["XK%d" % _i] = ("sbuf", [128, 4 * C], "bfloat16")
    SCRATCH["XC%d" % _i] = ("sbuf", [128, 4 * C], "bfloat16")
    SCRATCH["Z%d" % _i] = ("sbuf", [128, 4 * C], "bfloat16")
    SCRATCH["H%d" % _i] = ("sbuf", [128, 4 * E], "bfloat16")
    SCRATCH["B%d" % _i] = ("sbuf", [128, 4 * C], "bfloat16")
    SCRATCH["zq%d" % _i] = ("sbuf", [128, C1 + 256], F4)
    SCRATCH["zs%d" % _i] = ("sbuf", [128, C1 + 256], "uint8")
    SCRATCH["hq%d" % _i] = ("sbuf", [128, C1 + 128], F4)
    SCRATCH["hs%d" % _i] = ("sbuf", [128, C1 + 128], "uint8")
    SCRATCH["lq%d" % _i] = ("sbuf", [128, E], F4)
    SCRATCH["ls%d" % _i] = ("sbuf", [128, E], "uint8")
    SCRATCH["k4t%d" % _i] = ("sbuf", [128, 80], "uint16")
    SCRATCH["nf%d" % _i] = ("sbuf", [128, C], "float32")
    SCRATCH["kk%d" % _i] = ("sbuf", [128, C], "float32")
_ROWS = {
    "t16": 288, "t4": 288, "t8": 80, "t2": 80, "t32": 288, "J1": 80, "J2": 80, "q16": 16, "q32": 40, "m144": 288, "tmp": 288,
    "W1": 288, "W2": 288, "W3": 288, "W4": 288, "W5": 288, "cAD": 144, "sgM": 144, "M16n": 288, "M4n": 288, "M2": 80, "M8": 80,
    "m8z": 80, "d16": 80, "JM2": 80, "JM8": 80,
    "cT": 16, "tA": 16, "tB": 16, "tC": 16, "tD": 16, "tcAD": 16, "tcBC": 16, "sgT": 16, "tb": 16, "cc18": 16,
    "b1": 40, "cc4": 40, "bits": 288, "fl": 144, "BC": 16, "tw": 32, "ts": 32,
    "Vw": 80, "Vs": 80, "Vb": 80, "F0": 80, "F1": 80, "F2": 80, "G0": 80, "G1": 80, "G2": 80,
    "l0": 80, "l1": 80, "l2": 80, "l3": 80, "l4": 80, "l5": 80, "l6": 80, "l7": 80, "lc": 80,
    "fM2": 80, "dj": 40, "s1": 40, "fs": 40, "x4": 240, "z4": 216, "xs4": 216, "tab2": 40,
    "fM8": 80, "fS8": 80, "f18": 16, "s18": 16, "fs18": 16, "x8": 240, "z8": 216, "xs8": 216, "up": 16,
}
_ROWS2 = {
    "x2": 288, "z2": 288, "xs2": 288, "n4w": 288, "n4s": 288, "n16w": 288, "n16s": 288, "d4": 288, "d16b": 288,
    "Pw": 80, "Ps": 80, "Rw": 80, "Rs": 80, "Gw": 80, "Gs": 80, "fM4": 144, "fS4": 144, "m4z": 144,
}
OFF = {}
for _b, _t, _d in (("F", _ROWS, "float32"), ("G", _ROWS2, "bfloat16")):
    _n = 0
    for _k, _v in _t.items():
        OFF[_k] = (_b, _n, _v)
        _n += (_v + 15) // 16 * 16
    SCRATCH[_b] = ("sbuf", [128, _n], _d)

SEMAPHORES = ["v", "s", "p", "q", "sent", "dx0", "dx1", "dk", "du", "dw", "dv", "dkl", "dn1", "dn2", "df0", "df1", "df2", "dout",
              "lr0", "lr1", "lr2", "ha0", "ha1", "ha2", "hb0", "hb1", "hb2"]


def rank_program(g, core, T, topo):
    rank = T.rank_of(core)
    if rank is None:
        return
    A = AluOpType
    COPY, IDENT, SIGN = ActivationFunctionType.Copy, ActivationFunctionType.Identity, ActivationFunctionType.Sign
    queue = {"v": g.vector, "s": g.scalar, "p": g.tensor, "q": g, "y": g.sync}
    total, known, log = {}, {}, {}

    def f(name, a=0, b=None, step=1):
        o = OFF[name]
        return (o[0], o[1] + a, o[1] + (o[2] if b is None else b), step)

    def t(name, a=0, b=None, step=1):
        return (name, a, SCRATCH[name][1][1] if b is None else b, step)

    def ap(x):
        return T[x[0]][:, x[1]:x[2]:x[3]] if x[3] != 1 else T[x[0]][:, x[1]:x[2]]

    def ind(win, off):
        return ap(win).indirect(ap(off))

    def clash(x, y):
        if x[0] != y[0] or x[1] >= y[2] or y[1] >= x[2]:
            return False
        if x[3] == y[3] and x[3] > 1 and (x[1] - y[1]) % x[3]:
            return False
        return True

    def need(q, sem, val):
        if known.get((q, sem), 0) < val:
            queue[q].wait_ge(T.sem[sem], val)
            known[(q, sem)] = val

    def order(q, reads, writes):
        want = {}
        for rw, views in ((0, reads), (1, writes)):
            for x in views:
                for y, w, sem, val in log.get(x[0], ()):
                    if (rw or w) and clash(x, y):
                        want[sem] = max(want.get(sem, 0), val if val else total[sem])
        for sem in want:
            need(q, sem, want[sem])

    def note(sem, val, reads, writes):
        for x in writes:
            log[x[0]] = [e for e in log.get(x[0], []) if not (e[0][1] >= x[1] and e[0][2] <= x[2] and (x[3] == 1 or x == e[0]))]
            log[x[0]].append((x, 1, sem, val))
        for x in reads:
            log.setdefault(x[0], []).append((x, 0, sem, val))

    def run(q, call, reads, writes):
        psum = [("ps", x[1] // 512 * 512, x[1] // 512 * 512 + 512, 1) for x in reads + writes if x[0] == "ps"]
        reads, writes = [x for x in reads if x[0] != "ps"], [x for x in writes if x[0] != "ps"] + psum
        order(q, reads, writes)
        total[q] = total.get(q, 0) + 1
        call().then_inc(T.sem[q], 1)
        note(q, total[q], reads, writes)

    def dma(q, sem, out, in_, reads, writes):
        order(q, reads, writes)
        total[sem] = total.get(sem, 0) + 16
        queue[q].dma_start(out, in_).then_inc(T.sem[sem], 16)
        note(sem, 0, reads, writes)

    def tt(out, a, b, op):
        run("v", lambda: g.vector.tensor_tensor(ap(out), ap(a), ap(b), op), [a, b], [out])

    def ts(out, a, s1, op0, s2=None, op1=None):
        sc = [x for x in (s1, s2) if isinstance(x, tuple)]
        u1 = ap(s1) if isinstance(s1, tuple) else s1
        u2 = ap(s2) if isinstance(s2, tuple) else s2
        if op1 is None:
            run("v", lambda: g.vector.tensor_scalar(ap(out), ap(a), u1, None, op0), [a] + sc, [out])
        else:
            run("v", lambda: g.vector.tensor_scalar(ap(out), ap(a), u1, u2, op0, op1), [a] + sc, [out])

    def cp(out, a):
        run("v", lambda: g.vector.tensor_copy(ap(out), ap(a)), [a], [out])

    def gat(out, win, off):
        run("v", lambda: g.vector.tensor_copy(ap(out), ind(win, off)), [win, off], [out])

    def gop(out, win, off, b, op):
        run("v", lambda: g.vector.tensor_tensor(ap(out), ind(win, off), ap(b), op), [win, off, b], [out])

    def scan(out, d0, d1, op0, op1):
        run("v", lambda: g.vector.tensor_tensor_scan(ap(out), ap(d0), ap(d1), 0.0, op0, op1), [d0, d1], [out])

    def act(out, a, scale=1.0):
        run("s", lambda: g.scalar.activation(ap(out), ap(a), COPY, scale=scale), [a], [out])

    def acts(out, a, col):
        run("s", lambda: g.scalar.activation(ap(out), ap(a), COPY, scale=ap(col)), [a, col], [out])

    def actf(out, a, func, scale, bias):
        if isinstance(bias, tuple):
            run("s", lambda: g.scalar.activation(ap(out), ap(a), func, bias=ap(bias), scale=scale), [a, bias], [out])
        else:
            run("s", lambda: g.scalar.activation(ap(out), ap(a), func, bias=bias, scale=scale), [a], [out])

    def equal(out, a, col, tmp):
        actf(tmp, a, ActivationFunctionType.Abs, -1.0, col)
        actf(out, tmp, ActivationFunctionType.Relu, -1.0, 1.0)

    def actg(out, win, off, scale=1.0, bias=None):
        if bias is None:
            run("s", lambda: g.scalar.activation(ap(out), ind(win, off), COPY, scale=scale), [win, off], [out])
        else:
            run("s", lambda: g.scalar.activation(ap(out), ind(win, off), IDENT, bias=bias), [win, off], [out])

    def fill(out, c):
        run("v", lambda: g.vector.memset(ap(out), c), [], [out])

    def quant(q, s, a):
        run("v", lambda: g.vector.quantize_mx(ap(q), ap(s), ap(a)), [a], [q, s])

    def mm(out, l, ls, r, rs):
        run("p", lambda: g.tensor.matmul_mx(ap(out), ap(l), ap(ls), ap(r), ap(rs), True, True), [l, ls, r, rs], [out])

    def iota(out, pattern, base=0, cm=0):
        if out[0] == "F":
            run("q", lambda: g.iota(ap(out), pattern, base, cm, allow_small_or_imprecise_dtypes=True), [], [out])
        else:
            run("q", lambda: g.iota(ap(out), pattern, base, cm), [], [out])

    def bank(i, n):
        i %= 8
        return ("ps", 512 * i, 512 * i + n, 1)

    def send(dst, sem, out, in_, reads, bits=False):
        order("q", reads, [])
        rid, pid = topo.addr(dst, core)
        n = len(topo.engines(core, dst))
        o, i = (ap(out).bitcast(dt.uint8), ap(in_).bitcast(dt.uint8)) if bits else (ap(out), ap(in_))
        if SCRATCH[out[0]][0] == "dram":
            o, i = T[out[0]][:, :], T[in_[0]][:, :]
        total["sent"] = total.get("sent", 0) + n
        g.remote_dma(o, i, T.sem[sem], T.sem.sent, pid, rid, topo.mask(core, dst))
        return n

    def arrives(sem, n, writes):
        total[sem] = total.get(sem, 0) + n
        note(sem, 0, [], writes)

    dma("y", "dx0", T.X0[:, 0:640], T.x[:, 0:640], [], [t("X0", 0, 640)])
    dma("s", "dk", T.kli[:, :], T.kl[:, :], [], [t("kli")])
    dma("s", "du", T.ub[:, :], T.u[:, :], [], [t("ub")])
    dma("y", "dx1", T.X0[:, 640:1152], T.x[:, 640:1152], [], [t("X0", 640, 1152)])
    dma("y", "dkl", T.kld[:, :], T.kl[:, :], [], [t("kld")])
    need("y", "dx1", 16)
    dma("y", "dw", T.wq[:, 0:512].bitcast(dt.uint8), T.wc[:, :], [], [t("wq")])
    dma("y", "dw", T.wp[:, 0:512], T.ws[:, :], [], [t("wp")])
    dma("y", "dv", T.vb[:, :], T.v[:, :], [], [t("vb")])

    iota(t("pI", 0, 1), [[0, 1]], 0, 1)
    iota(t("uI"), [[16, 8]])
    iota(f("t16"), [[0, 18], [1, 16]])
    iota(f("q16", 0, 9), [[16, 9]])
    iota(f("t32"), [[0, 9], [1, 32]])
    iota(f("t2"), [[0, 40], [1, 2]])
    iota(f("t8"), [[0, 10], [1, 8]])
    iota(f("J1"), [[1, 80]], 1)
    iota(f("q32", 0, 36), [[32, 36]])
    for i, base in enumerate((72, 216, 1, 145)):
        iota(f("cAD", 36 * i, 36 * i + 36), [[2, 36]], base)
    iota(f("W1"), [[1, 288]])
    iota(f("t4"), [[0, 72], [1, 4]])
    partner = [T.cores[rank ^ m] for m in MASKS]
    arrives("lr0", send(partner[0], "lr0", t("lk0"), t("kld"), [t("kld")]), [t("lk0")])

    def pcol(i):
        return t("pF", i, i + 1)

    cp(t("uo"), t("uI"))
    ts(t("pI", 1, 2), t("pI", 0, 1), 15, A.bitwise_and)
    ts(t("pI", 2, 3), t("pI", 0, 1), 3, A.bitwise_and)
    ts(t("pI", 3, 4), t("pI", 0, 1), 15, A.bitwise_and, 2, A.arith_shift_right)
    ts(t("pI", 4, 5), t("pI", 0, 1), 15, A.bitwise_and, 3, A.arith_shift_right)
    ts(t("pI", 5, 6), t("pI", 0, 1), 15, A.bitwise_and, 1, A.arith_shift_right)
    ts(t("pI", 6, 7), t("pI", 0, 1), 2, A.arith_shift_right, 1, A.bitwise_and)
    ts(t("pI", 7, 8), t("pI", 0, 1), 1, A.bitwise_and)
    cp(t("pF", 0, 8), t("pI"))
    P16, P4, I4, I8, I2, PAR4, PAR2 = [pcol(i) for i in range(1, 8)]
    equal(f("M16n"), f("t16"), P16, f("tmp"))
    act(f("sgM", 0, 72), f("M16n", 0, 72))
    act(f("sgM", 72, 144), f("M16n", 72, 144), -1.0)
    actf(f("z2"), f("t32"), SIGN, 1.0, 0.0)
    actf(f("d16"), f("t16", 0, 80), SIGN, 1.0, 0.0)
    fill(f("x2"), 0.0)
    ts(f("cT", 0, 9), f("q16", 0, 9), P16, A.add)
    ts(f("tA", 0, 9), f("cT", 0, 9), 36.0, A.is_ge, 72.0, A.mult)
    ts(f("tB", 0, 9), f("cT", 0, 9), 108.0, A.is_ge, 72.0, A.mult)
    ts(f("tC", 0, 9), f("cT", 0, 9), 72.0, A.is_ge, 287.0, A.mult)
    ts(f("tD", 0, 9), f("cT", 0, 9), 2.0, A.mult, 72.0, A.add)
    tt(f("tA", 0, 9), f("tA", 0, 9), f("tB", 0, 9), A.add)
    tt(f("tD", 0, 9), f("tD", 0, 9), f("tC", 0, 9), A.subtract)
    ts(f("sgT", 0, 9), f("cT", 0, 9), 72.0, A.is_ge, -2.0, A.mult)
    ts(f("sgT", 0, 9), f("sgT", 0, 9), 1.0, A.add)
    tt(f("tcAD", 0, 9), f("tA", 0, 9), f("tD", 0, 9), A.add)
    tt(f("tcBC", 0, 9), f("tcAD", 0, 9), f("sgT", 0, 9), A.add)
    ts(f("x2", 31, 288, 32), f("tcAD", 0, 9), -144.0, A.add)

    def state(r, h):
        a, b = HS[h]
        quant(t("xq%d" % r, a, b), t("xs%d" % r, a, b), t("X%d" % r, 4 * a, 4 * b))

    def scores(r, h):
        a, b = HS[h]
        mm(bank(2 + h, b - a), t("ur"), t("urs"), t("xq%d" % r, a, b), t("xs%d" % r, a, b))

    fill(f("x4"), 0.0)
    fill(f("z4"), -1.0)
    fill(f("x8"), 0.0)
    fill(f("z8"), -1.0)
    quant(t("uq"), t("us"), t("ub"))
    state(0, 0)
    state(0, 1)
    run("v", lambda: g.vector.tensor_copy(T.ur[:, 0:128].bitcast(dt.uint32), T.uq[:, 0:128].bitcast(dt.uint32).indirect(T.uo[:, 0:8])),
        [t("uq"), t("uo")], [t("ur")])
    run("s", lambda: g.scalar.activation(T.urs[:, 0:128], T.us[:, 0:128].indirect(T.uo[:, 0:8]), COPY), [t("us"), t("uo")], [t("urs")])

    def ends(n):
        act(f(n, 0, 72), f("W1", 0, 72))
        act(f(n, 216, 288), f("W1", 216, 288))

    actf(f("d16"), f("d16"), IDENT, 16384.0, -8192.0)
    actf(f("M16n"), f("M16n"), IDENT, 4096.0, -4096.0)
    ends("W2")
    act(f("d16b", 0, 80), f("d16"))
    ends("W3")
    act(f("J2"), f("J1"))

    scores(0, 0)
    scores(0, 1)
    cp(t("kt0"), t("kli"))
    for e in range(4):
        ts(t("k4t0", 20 * e, 20 * e + 18), t("kli"), 4, A.mult, e, A.add)
    run("v", lambda: g.vector.memset(T.one[:, 0:512], 1.0), [], [t("one")])
    for e in range(4):
        run("q", lambda: g.affine_select(T.et[:, 512 * e:512 * e + 512], T.one[:, 0:512], [[-1, 512]], A.is_equal, 0.0, e, 4),
            [t("one")], [t("et", 512 * e, 512 * e + 512)])

    def constants2():
        ts(t("pF", 16, 20), f("t4", 0, 4), I4, A.is_equal, 4.0, A.mult)
        ts(t("pF", 20, 22), f("t4", 0, 2), I8, A.is_equal)
        ts(t("pF", 9, 11), t("pF", 6, 8), -2.0, A.mult, 1.0, A.add)
        ts(pcol(13), I4, 0.0, A.is_equal)
        ts(pcol(8), I4, 8.0, A.mult, P4, A.add)
        ts(pcol(12), P16, 15.0, A.is_equal)
        tt(f("JM2"), f("J1"), f("M2"), A.mult)
        tt(f("JM2", 0, 1), f("JM2", 0, 1), pcol(13), A.subtract)
        actf(f("b1", 0, 36), f("q32", 0, 36), IDENT, 1.0, pcol(8))
        actf(f("cc4", 0, 36), f("b1", 0, 36), IDENT, 2.0, 4.0)

    def constants3():
        ts(pcol(14), P16, 0.0, A.is_equal)
        tt(f("JM8"), f("J1"), f("M8"), A.mult)
        tt(f("JM8", 0, 1), f("JM8", 0, 1), pcol(14), A.subtract)

    def constants4():
        ts(f("tmp"), f("t16"), 0.0, A.is_gt, 16384.0, A.mult)
        ts(f("d16b"), f("tmp"), -8192.0, A.add)

    def table(out, src, n, step=16):
        cp(out, (src[0], src[1] + step - 1, src[1] + n, step))

    for r in range(3):
        X, XK, XC, Z, H, B, kt = ["%s%d" % (n, r) for n in ("X", "XK", "XC", "Z", "H", "B", "kt")]
        zq, zs, hq, hs, lq, ls, nf, kk = ["%s%d" % (n, r) for n in ("zq", "zs", "hq", "hs", "lq", "ls", "nf", "kk")]
        kf, lk = "kf%d" % r, "lk%d" % r
        for i in range(16):
            dma("y", "df%d" % r, T[kf][i:128:16, :], T[lk][:, :], [t(lk)], [(kf, i, C, 16)])
        for h in range(2):
            ts(f("bits", HS[h][0], HS[h][1]), bank(2 + h, HS[h][1] - HS[h][0]), 0.0, A.is_gt)
        actg(f("fl"), f("bits"), t(kt, 0, 9))

        def half_of_xk(h):
            for e in (2 * h, 2 * h + 1):
                actg(t(XK, e, 1152, 4), t(X), t("k4t%d" % r, 20 * e, 20 * e + 18), 0.5)

        half_of_xk(0)
        if r == 0:
            ends("W4")
            ends("W5")
            for m, c, i, o in (("M2", "t2", I8, 0), ("M8", "t8", I2, 80)):
                equal(f(m), f(c), i, f("tmp", o, o + 80))
            actf(f("m4z"), f("t4", 0, 144), SIGN, 1.0, 0.0)
        gop(f("x2", 0, 288, 2), f("bits"), t(kt, 0, 9), f("sgM"), A.mult)
        scan(f("xs2"), f("z2"), f("x2"), A.mult, A.add)
        sd = f("xs2", 30, 288, 32)
        ts(t("oAD", 0, 9), f("xs2", 31, 288, 32), 144.0, A.add)
        tt(f("BC", 0, 9), f("tcBC", 0, 9), sd, A.subtract)
        tt(f("W1", 72, 144), f("cAD", 0, 72), f("fl", 0, 72), A.add)
        tt(f("W1", 144, 216), f("cAD", 72, 144), f("fl", 72, 144), A.subtract)
        cp(t("oBC", 0, 9), f("BC", 0, 9))
        gat(f("W2", 72, 216), f("W1"), t("oAD", 0, 9))
        ts(t("oRi", 0, 5), f("BC", 0, 5), -72.0, A.add, 0.0, A.max)
        gat(f("W3", 72, 216), f("W2"), t("oAD", 0, 9))
        if r == 0:
            constants2()
        gop(f("tw", 0, 16), f("W3"), t("oAD", 0, 1), f("M16n", 0, 16), A.add)
        gop(f("tw", 16, 32), f("W3"), t("oAD", 8, 9), f("M16n", 0, 16), A.add)
        def masks():
            for i in range(4):
                acts(f("fM4", i, 144, 4), f("fl", i, 144, 4), pcol(16 + i))
            act(f("fM4", 143, 144), pcol(19))
            for i in range(2):
                acts(f("fM2", i, 72, 2), f("fl", i, 72, 2), pcol(20 + i))
        if r > 0:
            masks()
        actg(f("W4", 72, 216), f("W3"), t("oAD", 0, 9))
        actg(f("W5", 72, 216), f("W3"), t("oAD", 0, 9))
        if r == 0:
            masks()
        def late():
            actf(f("m144"), f("t16"), IDENT, 0.0, -144.0)
            actf(f("z4", 0, 216, 6), f("q32", 0, 36), IDENT, 0.0, 0.0)
            actf(f("z4", 2, 216, 6), f("q32", 0, 36), IDENT, 0.0, 1.0)
            actf(f("z8", 2, 216, 3), f("t2", 0, 72), IDENT, 0.0, 1.0)
            actf(f("z8", 0, 216, 24), f("q16", 0, 9), IDENT, 0.0, 0.0)
            actf(f("m8z"), f("t8"), SIGN, 1.0, 0.0)
            actf(f("tb", 0, 9), f("cT", 0, 9), IDENT, 2.0, 0.0)
            actf(f("cc18", 0, 9), f("cT", 0, 9), IDENT, 4.0, 1.0)
        if r > 0:
            half_of_xk(1)
        scan(f("ts"), f("d16", 0, 32), f("tw"), A.min, A.max)
        cp(t("o4", 0, 4, 2), f("ts", 15, 32, 16))
        if r > 0:
            scan(f("fS4"), f("m4z"), f("fM4"), A.mult, A.add)
        gat(f("W5", 72, 88), f("W4"), t("o4", 0, 1))
        gat(f("W5", 200, 216), f("W4"), t("o4", 2, 3))
        if r == 0:
            scan(f("fS4"), f("m4z"), f("fM4"), A.mult, A.add)
        tt(f("dj", 0, 36), f("fM2", 0, 72, 2), f("fM2", 1, 72, 2), A.add)
        gop(f("Vw"), f("W5"), t("oBC", 0, 5), f("M16n", 0, 80), A.add)
        actg(f("Vb"), f("W5"), t("oBC", 4, 9))
        ts(f("s1", 0, 36), f("fS4", 3, 144, 4), -2.0, A.mult, 4.0, A.add)
        scan(f("Vs"), f("d16"), f("Vw"), A.min, A.max)
        gop(f("Rw"), f("W5"), t("oRi", 0, 5), f("M16n", 0, 80), A.add)
        ts(t("oVC", 0, 5), f("Vs", 15, 80, 16), -208.0, A.add, 8.0, A.max)
        scan(f("Rs"), f("d16b", 0, 80), f("Rw"), A.min, A.max)
        ts(f("fs", 0, 36), f("dj", 0, 36), pcol(9), A.mult, PAR4, A.add)
        gop(f("Pw"), f("Vb"), t("oVC", 0, 5), f("M16n", 0, 80), A.add)
        actg(f("F0"), f("Vb"), t("oVC", 0, 5))
        if r == 0:
            late()
        tt(f("x4", 5, 216, 6), f("b1", 0, 36), f("fS4", 3, 144, 4), A.add)
        scan(f("Ps"), f("d16b", 0, 80), f("Pw"), A.min, A.max)
        ts(t("oR", 0, 5), f("Rs", 15, 80, 16), 71.0, A.min)
        table(t("oP0", 0, 5), f("Ps"), 80)
        low = f("J1")
        for i in range(4):
            o = t("oP%d" % i, 0, 5)
            Fi, Gi, la, lb = f("F%d" % (i % 3)), f("G%d" % (i % 3)), f("l%d" % (2 * i)), f("l%d" % (2 * i + 1))
            if i < 3:
                gat(Gi, Fi, o)
            if i == 0:
                gop(la, low, o, f("J2"), A.min)
            else:
                gop(la, low, o, f("lc"), A.min)
            if i < 3:
                gop(f("Gw"), Gi, o, f("M16n", 0, 80), A.add)
                gop(lb, la, o, low, A.min)
                if i < 2:
                    actg(f("F%d" % (i + 1)), Gi, o)
                act(f("lc"), lb)
                if r == 0 and i < 2:
                    actg(t(XK, 2 + i, 1152, 4), t(X), t("k4t0", 40 + 20 * i, 58 + 20 * i), 0.5)
                if i == (1 if r else 2):
                    act(t(XC, 0, 576), t(XK, 0, 576))
                if i == 2:
                    act(t(XC, 576, 1152), t(XK, 576, 1152))
                scan(f("Gs"), f("d16b", 0, 80), f("Gw"), A.min, A.max)
                if i == 0:
                    tt(f("z4", 5, 216, 6), f("s1", 0, 36), f("fs", 0, 36), A.mult)
                elif i == 1:
                    tt(f("f18", 0, 9), sd, f("sgT", 0, 9), A.mult)
                else:
                    ts(f("s18", 0, 9), f("f18", 0, 9), -2.0, A.mult, 1.0, A.add)
                table(t("oP%d" % (i + 1), 0, 5), f("Gs"), 80)
                if i == 0:
                    tt(f("fM8", 0, 72), f("fl", 0, 72), f("M8", 0, 72), A.mult)
                elif i == 1:
                    tt(f("f18", 8, 9), f("f18", 8, 9), pcol(12), A.max)
                else:
                    scan(f("fS8", 0, 72), f("m8z", 0, 72), f("fM8", 0, 72), A.mult, A.add)
            else:
                tt(f("x8", 23, 216, 24), f("tb", 0, 9), f("f18", 0, 9), A.add)
                gop(lb, la, o, f("lc"), A.min)
            low = lb
        ts(f("fs18", 0, 9), f("fS8", 7, 72, 8), pcol(10), A.mult, PAR2, A.add)
        gop(f("x4", 0, 240, 3), low, t("oR", 0, 5), f("JM2"), A.is_equal)
        tt(f("x4", 1, 216, 3), (low[0], low[1], low[1] + 72, 1), f("JM2", 0, 72), A.is_equal)
        tt(f("z8", 23, 216, 24), f("fs18", 0, 9), f("s18", 0, 9), A.mult)
        scan(f("xs4"), f("z4"), f("x4", 0, 216), A.mult, A.add)
        cp(t("tt4", 0, 36), f("xs4", 5, 216, 6))
        tt(f("tab2", 0, 36), f("cc4", 0, 36), f("xs4", 5, 216, 6), A.subtract)
        if r > 0:
            actg(t(kk), t("kf%d" % r), t(kt), 1.0, -144.0)

        def layer(i, a, b, at):
            gop(t(Z, 4 * a, 4 * b), t(XK), t("tt4", a // 4, b // 4), t(XC, 4 * a, 4 * b), A.add)
            if i == 0:
                cp(t("tt4", 36, 72), f("tab2", 0, 36))
            n = max(128, b - a)
            p = 0 if i == 0 else C1 + 128 * (i - 1)
            q, s = t(zq, p, p + n), t(zs, p, p + n)
            quant(q, s, t(Z, 4 * (b - n), 4 * b))
            for k in range(4):
                mm(bank(at + k, n), t("wq", 128 * k, 128 * k + 128), t("wp", 128 * k, 128 * k + 128), q, s)
                o, c = bank(at + k, n), t(B, C * k + a, C * k + b) if i == 2 else t(H, 4 * a + k, 4 * b, 4)
                act(c, (o[0], o[2] - (b - a), o[2], 1), 0.03125)

        layer(0, 0, C1, 4)
        layer(1, C1, E, 8)
        quant(t(hq, 0, C1), t(hs, 0, C1), t(H, 0, 4 * C1))
        dst = partner[r]
        n = send(dst, "ha%d" % r, t(lq, 0, C1), t(hq, 0, C1), [t(hq, 0, C1)], True)
        n += send(dst, "ha%d" % r, t(ls, 0, C1), t(hs, 0, C1), [t(hs, 0, C1)])
        if r == 0:
            constants3()
        tt(f("x8", 1, 216, 3), (low[0], low[1], low[1] + 72, 1), f("JM8", 0, 72), A.is_equal)
        gop(f("x8", 0, 240, 3), low, t("oR", 0, 5), f("JM8"), A.is_equal)
        quant(t(hq, C1, C1 + 128), t(hs, C1, C1 + 128), t(H, 4 * (E - 128), 4 * E))
        m = send(dst, "hb%d" % r, t(lq, C1, E), t(hq, C1 + 128 - C2, C1 + 128), [t(hq, C1, C1 + 128)], True)
        m += send(dst, "hb%d" % r, t(ls, C1, E), t(hs, C1 + 128 - C2, C1 + 128), [t(hs, C1, C1 + 128)])
        arrives("ha%d" % r, n, [t(lq, 0, C1), t(ls, 0, C1)])
        arrives("hb%d" % r, m, [t(lq, C1, E), t(ls, C1, E)])
        scan(f("xs8"), f("z8"), f("x8", 0, 216), A.mult, A.add)
        layer(2, E, C, 12)
        if r == 0:
            constants4()
        tt(f("up", 0, 9), f("cc18", 0, 9), f("xs8", 23, 216, 24), A.subtract)
        cp(t("tt18", 0, 9), f("xs8", 23, 216, 24))
        cp(t("tt18", 9, 18), f("up", 0, 9))
        if r == 0:
            ts(t("ki", 0, 18), t("kli"), 15, A.bitwise_and)
            ts(t("ki", 18, 36), t("kli"), 4, A.arith_shift_right)
            ts(t("ki", 0, 18), t("ki", 0, 18), 18, A.mult)
            tt(t("ki", 36, 54), t("ki", 0, 18), t("ki", 18, 36), A.add)
            cp(t("ks"), t("ki", 36, 54))
            gop(t(kk), t(kf), t("ks"), f("m144"), A.add)
        gop(f("n16w"), t(kk), t("tt18"), f("M16n"), A.add)
        actg(t(nf), t(kk), t("tt18"), 1.0, 144.0)
        scan(f("n16s"), f("d16b"), f("n16w"), A.min, A.max)
        ts(t("kt%d" % (r + 1)), f("n16s", 15, 288, 16), 144.0, A.add)
        if r < 2:
            for e in range(4):
                ts(t("k4t%d" % (r + 1), 20 * e, 20 * e + 18), f("n16s", 15, 288, 16), 4.0, A.mult, 576.0 + e, A.add)
            nd = "nd%d" % (r + 1)
            dma("y", "dn%d" % (r + 1), T[nd][:, :], T[nf][0:128:16, :], [t(nf)], [t(nd)])
            lr = "lr%d" % (r + 1)
            arrives(lr, send(partner[r + 1], lr, t("lk%d" % (r + 1)), t(nd), [t(nd)]), [t("lk%d" % (r + 1))])
        else:
            dma("y", "dout", T.kp[:, :], T[nf][0:128:16, :], [t(nf)], [])
        if r == 0:
            quant(t("eq"), t("es"), t("et"))
            quant(t("vq"), t("vs"), t("vb"))
        for c0, c1, new, at in ((0, C1, 0, 16), (E - 128, E, 128 - C2, 20)):
            for b in range(4):
                mm(bank(at + b, c1 - c0), t("eq", 128 * b, 128 * b + 128), t("es", 128 * b, 128 * b + 128), t(lq, c0, c1), t(ls, c0, c1))
                k = bank(at + b, c1 - c0)
                k = (k[0], k[1] + new, k[2], 1)
                act(t(B, C * b + c0 + new, C * b + c1), k)
        Xn = "X%d" % (r + 1)
        for e, a, b in ((0, 0, C), (1, 0, C), (2, 0, C), (3, 0, HS[0][1]), (3, HS[1][0], C)):
            gop(t(Xn, 4 * a + e, 4 * b, 4), t(B, C * e, C * e + C), t("kt%d" % (r + 1), a // 16, b // 16), t(X, 4 * a + e, 4 * b, 4), A.add)
        for h in range(2):
            state(r + 1, h)
            if r < 2:
                scores(r + 1, h)
            if r == 2:
                q, s = "xq3", "xs3"
                a, b = HS[h]
                mm(bank(2 + h, b - a), t("vq"), t("vs"), t(q, a, b), t(s, a, b))
                dma("y", "dout", T.oc[:, 4 * a:4 * b], T[q][:, a:b].bitcast(dt.uint8), [t(q, a, b)], [])
                for i in range(4):
                    dma("y", "dout", T.osc[4 * i:4 * i + 4, a:b], T[s][32 * i:32 * i + 4, a:b], [t(s, a, b)], [])
                act(t("ysb", a, b), bank(2 + h, b - a))
                dma("s", "dout", T.y[:, a:b], T.ysb[:, a:b], [t("ysb", a, b)], [])
    need("y", "dout", total["dout"])
    need("q", "sent", total["sent"])
    for sem in ("v", "s", "p", "q"):
        need("y", sem, total[sem])
